import numpy as np, ml_dtypes
CORES = [16,17,18,19,32,33,34,35]
N = 8
import mx_ref
BF = ml_dtypes.bfloat16
def gentries(a):
    return np.ascontiguousarray(a.reshape(8, 16, -1).transpose(0, 2, 1)).reshape(8, -1)
def gtable(e):
    e = np.asarray(e); return np.ascontiguousarray(e.reshape(8, -1, 16).transpose(0, 2, 1)).reshape(128, -1).astype(np.int32)
def gcols(t, e):
    v = np.concatenate([t.reshape(8, 16, -1, 4), np.zeros((8, 16, 1, 4), BF)], axis=2)
    return np.ascontiguousarray(np.stack([v[g][:, e[g]] for g in range(8)])).reshape(128, -1)
def tile(rs):
    return np.stack(rs, axis=2).reshape(128, -1).astype(BF)
def pick(q, e):
    c = np.concatenate([q[0].reshape(128, -1, 4), np.zeros((128, 1, 4), np.uint8)], axis=1); s = np.concatenate([q[1], np.ones((16, 1), np.uint8)], axis=1)
    return (np.ascontiguousarray(c[:, e].reshape(128, -1)), np.ascontiguousarray(s[:, e]))
def join(*qs):
    return (np.concatenate([q[0] for q in qs], axis=1), np.concatenate([q[1] for q in qs], axis=1))
def put(q, e, v):
    c, s = q[0].reshape(128, -1, 4).copy(), q[1].copy(); c[:, e] = v[0].reshape(128, -1, 4); s[:, e] = v[1]
    return (c.reshape(128, -1), s)
def pk(c, s):
    return (np.ascontiguousarray(c), mx_ref.live(s))
def emit(q):
    return q[0], q[1]
def packed(v, rng):
    q = [mx_ref.quantize(np.ascontiguousarray(v[r])) for r in range(N)]
    return np.stack([a for a, b in q]), np.stack([mx_ref.plane(b, rng) for a, b in q])
def values_of_codes():
    e, c = np.zeros((128, 128, 4), np.float32), np.zeros((128, 2, 4), np.uint8)
    e[np.arange(128), np.arange(128), 0] = 1
    c[:127, :, 0] = np.arange(256).reshape(2, 128).T[:127]
    return mx_ref.matmul(mx_ref.quantize(e.reshape(128, 512).astype(BF)), (c.reshape(128, 8), np.full((16, 2), 127, np.uint8))).T.reshape(-1).astype(np.float64)
CODE_VALUE, SCALE_VALUE = values_of_codes(), 2.0 ** (np.arange(256) - 127.0)
def decode(q):
    return (CODE_VALUE[q[0]].reshape(16, 8, -1, 4) * SCALE_VALUE[q[1]][:, None, :, None] + 0.0).reshape(128, -1).astype(np.float32)
def f(rng, *shape):
    return mx_ref.flush((rng.standard_normal(shape, dtype=np.float32) * np.exp2(rng.integers(-2, 3, shape[:-1] + (1,)))).astype(BF))
def wide(rng, *shape, cols=0):
    v = rng.standard_normal(shape, dtype=np.float32) * np.exp2(rng.integers(-12, 13, shape)).astype(np.float32)
    if cols: v *= np.repeat(np.exp2(rng.integers(-cols, cols + 1, shape[:-2] + (1, shape[-1] // 4))) * (rng.random(shape[:-2] + (1, shape[-1] // 4)) > 0.0625), 4, axis=-1).astype(np.float32)
    return mx_ref.flush(v.astype(BF))
C, H = 320, 160
STEP = [1, 2, 4]
def numbers_of(rng):
    return {"x": np.array(f(rng, N, 128, 4 * C)), "u": np.array(f(rng, N, 128, 512)), "v": np.array(f(rng, N, 128, 512))}
def stored(m):
    return {"ml": np.stack([gtable(m[r]) for r in range(N)])}
def paired(e):
    m = np.zeros_like(e)
    np.put_along_axis(m, e, np.roll(e, H, axis=-1), axis=-1)
    return m
def pairings(rng):
    return paired(rng.permuted(np.tile(np.arange(C), (N, 8, 1)), axis=2))
def zigzag(rng, loop):
    s, t = rng.permutation(H), rng.permutation(H)
    a = np.concatenate([np.roll(t, -1), H + np.roll(s, -1)]).reshape(-1, 2)
    if not loop: a[H // 2 - 1, 1], a[-1, 0] = int(a[-1, 0]), int(a[H // 2 - 1, 1])
    b = np.concatenate([s, H + t]).reshape(-1, 2)
    return [paired(np.concatenate([k[:, 0], k[:, 1]])) for k in (a, b)]
def coil(rng):
    s = rng.permutation(H)
    k = np.concatenate([s, H + np.roll(s[:-1], -1), H + s[-1:]]).reshape(-1, 2)
    k[H // 2 - 1, 1], k[-1, 0] = int(k[-1, 0]), int(k[H // 2 - 1, 1])
    return paired(np.concatenate([k[:, 0], k[:, 1]]))
def layers(rng, still=[], pairs=False):
    w = np.array(f(rng, N, 128, 2048)).reshape(N, 8, 16, 4, 8, 16, 4)
    for i in still:
        w[:, :, i] = 0
        w[:, :, :, :, :, i] = 0
    if pairs:
        w[:, :, :, :, :, 8:] = 0
        for g in range(8):
            w[:, g, 8, 0, g, 8, 0] = -28.0
            for b in range(4): w[:, g, 10, b, g, 9, 0] = -2.0 ** (b - 5)
    return w
def weights(rng, w):
    c, s = packed(np.ascontiguousarray(w).reshape(N, 128, 2048), rng)
    return {"wc": c, "ws": s}
def setup_inputs(rng):
    return {**numbers_of(rng), **stored(pairings(rng)), **weights(rng, layers(rng))}
def setup_inputs_ties(rng):
    d = numbers_of(rng)
    o = rng.permutation(N)
    k = rng.integers(0, 4, (N, 8, C))
    k[o[0]] = 0
    k[o[1]] -= 4
    k[o[2]] = np.arange(C) < H
    kind = rng.permutation(8)
    m = np.zeros((N, 8, C), np.int64)
    for g in range(8):
        if 4 <= kind[g] < 7: k[:, g] = np.sort(k[:, g].reshape(N, 2, H), axis=1).reshape(N, C)
        for r in range(N):
            p, q = r ^ STEP[0], r ^ STEP[1]
            if kind[g] < 4 and r < p:
                a = zigzag(rng, kind[g] == 3)
                j = int(rng.integers(2))
                m[r, g], m[p, g] = a[j], a[1 - j]
            if 4 <= kind[g] < 6 and r < min(p, q, p ^ STEP[1]):
                m[r, g], m[q, g] = zigzag(rng, False)
                m[p, g] = m[p ^ STEP[1], g] = paired(np.arange(C))
            if kind[g] == 7: m[r, g] = paired(np.concatenate([rng.permutation(H), H + rng.permutation(H)]))
        if kind[g] == 6:
            m[:, g] = paired(np.arange(C))
            r = int(rng.integers(N))
            if STEP[0] ^ STEP[1] == STEP[2]: m[r, g] = coil(rng)
            else: m[r, g], m[r ^ STEP[2], g] = zigzag(rng, False)
    x = d["x"].reshape(N, 8, 16, C, 4)
    x[:, :, 0] = 0
    x[:, :, 0, :, 0] = k.astype(np.float32).astype(BF)
    a = np.exp2(rng.integers(-3, 4, (N, 8, 1)).astype(np.float32))
    x[:, :, 8:] = 0
    x[:, :, 8, :, 0] = (-1.125 * a).astype(BF)
    x[:, :, 10, :, 0] = (-0.0703125 * a).astype(BF)
    u = d["u"].reshape(N, 128, 128, 4)
    u[:, :, ::16] = 0
    for h in range(0, 128, 16): u[:, h, h, 0] = 1.0
    return {"x": x.reshape(N, 128, 4 * C), "u": u.reshape(N, 128, 512), "v": d["v"], **stored(twist(k, m)), **weights(rng, layers(rng, [0], True))}
def setup_inputs_near(rng):
    d = numbers_of(rng)
    x = d["x"].astype(np.float32).reshape(N, 8, 16, C, 4)
    x[:, :, 0] = 0
    x[:, :, 8:] = 0
    u = d["u"].reshape(N, 128, 128, 4)
    u[:, :, ::16] = 0
    w = layers(rng, [0, 8, 9, 10, 11, 12, 13, 14, 15])
    o = rng.permutation(N) % 4
    for r in range(N):
        c = rng.choice([-1.0, 1.0], (8, 1))
        s = rng.integers(0, 16, (8, C))
        digits = ((s[:, :, None] >> np.arange(4)) & 1) * np.exp2(np.arange(4) - 23.0)
        if o[r] < 2:
            x[r, :, 0, :, 0] = c
            x[r, :, 8] = digits
            x[r, :, 11, :, 0] = 2.0 ** -10
        elif o[r] == 2: x[r, :, 8] = digits * rng.choice([-1.0, 1.0], (8, C, 1))
        else:
            x[r, :, 8, :, 0] = np.where(s < 8, 1.25, 0.0) * 2.0 ** -30 * c
            x[r, :, 9, :, 0] = np.where(s < 8, 0.0, 1.125) * 2.0 ** -30 * c
            for g in rng.permutation(8)[:4]:
                e = rng.choice([-1.0, 1.0], C) * 2.0 ** -30
                x[r, g, 8, :, 0] = 1.25 * e
                x[r, g, 9, :, 0] = -1.125 * e
            for g in range(8):
                w[r, g, 8, 0, g, 12, 0] = 2.0 ** -8
                w[r, g, 8, 0, g, 14, 0] = 64.0
                w[r, g, 1, 0, g, 2, 0] = 256.0
        at = [0, C - 1, int(rng.integers(C)), int(rng.integers(C))]
        for g, j in zip(rng.permutation(8)[:4], at): x[r, g, 0, j, 0] = 2.0 ** 29 * rng.choice([-1.0, 1.0])
        k = 1.0 if o[r] == 0 else 2.0 ** -30
        for h in range(0, 128, 16):
            u[r, h, h, 0] = k if o[r] < 2 else 1.0
            if o[r] < 2: u[r, h + 11, h, 0] = k
            if o[r] < 3: u[r, h + 8, h] = k
            else:
                u[r, h + 8, h, 0] = k
                u[r, h + 9, h, 0] = 1.125 * k
                u[r, h + 12, h, 0] = k
    return {"x": x.reshape(N, 128, 4 * C).astype(BF), "u": u.reshape(N, 128, 512), "v": d["v"], **stored(pairings(rng)), **weights(rng, w)}
def setup_inputs_odd(rng):
    d = numbers_of(rng)
    x = (1.0 + (2 * rng.integers(0, 64, (N, 16, 8, C, 4)) + 1) * 2.0 ** -7) * np.exp2(-rng.integers(0, 7, (N, 16, 8, C, 4)).astype(np.float64)) * rng.choice([-1.0, 1.0], (N, 16, 8, C, 4))
    x[:, :, 0, :, 0] = 1.96875 * 2.0 ** 8 * rng.choice([-1.0, 1.0], (N, 16, C))
    u = d["u"].reshape(N, 16, 8, 128, 4)
    u[:, :, 0, ::16] = 0
    for r in range(N):
        for i, g in enumerate(rng.permutation(8)[:4]):
            x[r, 2 * g, 1, :, 0] = (8 + rng.integers(0, 2, C)) * 2.0 ** (i - 8)
            u[r, :, :, 16 * g] = 0
            u[r, 2 * g, 1, 16 * g, 0] = 1.0
    return {"x": x.astype(np.float32).reshape(N, 128, 4 * C).astype(BF), "u": u.reshape(N, 128, 512), "v": d["v"], **stored(pairings(rng)), **weights(rng, layers(rng, [0, 8]))}
def setup_inputs_ends(rng):
    d = numbers_of(rng)
    x = np.zeros((N, 8, 16, C, 4))
    u = d["u"].astype(np.float32).reshape(N, 128, 128, 4)
    v = d["v"].astype(np.float32)
    w = np.zeros((N, 128, 4, 128, 4), np.float32)
    m = pairings(rng)
    o, e = rng.permutation(N) % 4, rng.permutation(N) % 4
    i = np.arange(128)
    for r in range(N):
        h = rng.permutation(8)
        c = np.where(h < 2, 0.0, h % 2 * 2.0 - 1.0)[None, :, None]
        k = np.array([2.0, 4.0, -4.0])[rng.permutation(8) % 3]
        low = -(0.9 + 0.1 * rng.random((8, 16, C, 4))) * 2.0 ** 28
        if o[r] == 0: x[r] = low
        if o[r] == 1: x[r] = low * rng.choice([-1.0, 1.0], (C, 1))
        if o[r] < 2:
            u[r, :, ::16] = c * (0.9 + 0.1 * rng.random((128, 8, 4))) * 2.0 ** 30
            v[r] = rng.choice([-1.0, 1.0], (128, 512)) * (0.9 + 0.1 * rng.random((128, 512))) * 2.0 ** 30
        if o[r] == 2:
            x[r] = -(1.0 + 0.125 * rng.integers(0, 8, (8, 16, C, 4))) * 2.0 ** -30
            u[r, :, ::16] = c * (1.0 + 0.125 * rng.integers(0, 8, (128, 8, 4))) * 2.0 ** -30
            v[r] = rng.choice([-1.0, 1.0], (128, 512)) * (1.0 + 0.125 * rng.integers(0, 8, (128, 512))) * 2.0 ** -30
            k[:] = 32.0
        if o[r] == 3:
            x[r] = d["x"][r].astype(np.float32).reshape(8, 16, C, 4)[:, :, :1]
            u[r, :, ::16] *= np.abs(c).astype(np.float32)
        for b in range(4): w[r, i, b, i, b] = k[i // 16]
        if e[r] < 3: m[r] = [paired(np.arange(C)), np.arange(C) ^ 1, C - 1 - np.arange(C)][e[r]]
    return {"x": x.astype(np.float32).reshape(N, 128, 4 * C).astype(BF), "u": u.reshape(N, 128, 512).astype(BF), "v": v.astype(BF), **stored(m), **weights(rng, w.astype(BF))}
def setup_inputs_spread(rng):
    d = setup_inputs(rng)
    d["x"] = wide(rng, N, 128, 4 * C, cols=6)
    return d
def check_inputs(d):
    b = []
    for k in ("x", "u", "v"):
        a = np.abs(d[k].astype(np.float32))
        if not (np.isfinite(a).all() and ((a == 0) | (a >= 2.0 ** -30) & (a <= 2.0 ** 30)).all()): b.append("a value of " + k)
    none, least, most = [emit(mx_ref.quantize(np.full((128, 16), k, np.float32).astype(BF)))[1][0, 0] for k in (0.0, 2.0 ** -8, 2.0 ** 8)]
    for r in range(N):
        e = gentries(d["ml"][r]).astype(np.int64)
        if not ((e >= 0) & (e < C)).all(): b.append("an entry of ml")
        elif (e == np.arange(C)).any() or (np.take_along_axis(e, e, axis=1) != np.arange(C)).any(): b.append("ml: not a pairing")
        if ((d["wc"][r] == 0x7F) | (d["wc"][r] == 0xFF)).any(): b.append("wc: a code that is no number")
        s = mx_ref.live(d["ws"][r])
        if ((s != none) & ((s < least) | (s > most))).any(): b.append("ws: a scale out of range")
    return b
def twist(s, m):
    e = np.zeros(m.shape, np.int64) + np.arange(C)
    swap = H * (s[..., :H] > s[..., H:])
    e[..., :H] += swap
    e[..., H:] -= swap
    return np.take_along_axis(e, np.take_along_axis(m, e, axis=-1), axis=-1)
def glued(a, b):
    at = np.tile(np.arange(C), (8, 1))
    far = at >= H
    done = np.zeros((8, C), bool)
    for _ in range(H + 1):
        at = np.where(done, at, np.where(far, np.take_along_axis(b, at, axis=1), np.take_along_axis(a, at, axis=1)))
        done = done | ((at >= H) == far)
        at = np.where(done, at, np.where(far, at + H, at - H))
        far = far ^ ~done
        if done.all(): break
    return at
def plus(s, t):
    return (s.astype(np.float32) + t.astype(np.float32)).astype(BF)
def reference(x, u, v, ml, wc, ws):
    qu = [mx_ref.quantize(u[r]) for r in range(N)]
    lay = [pk(wc[r], ws[r]) for r in range(N)]
    now = [x[r] for r in range(N)]
    mate = [gentries(ml[r]).astype(np.int64) for r in range(N)]
    for step in STEP:
        turned, qa = [], []
        for r in range(N):
            s = mx_ref.matmul(qu[r], mx_ref.quantize(now[r]))[::16] + np.float32(0.0)
            turned.append(twist(s, mate[r]))
            qz = mx_ref.quantize(plus(now[r], gcols(now[r], turned[r])))
            qa.append(mx_ref.quantize(tile([mx_ref.matmul(pick(lay[r], np.arange(128 * b, 128 * b + 128)), qz) * np.float32(0.015625) for b in range(4)])))
        made = []
        for r in range(N):
            p = r ^ step
            mate[r] = glued(turned[r], turned[p])
            t = decode(join(pick(qa[r], np.arange(H)), pick(qa[p], np.arange(H, C)))).astype(BF)
            made.append(plus(now[r], gcols(t, mate[r])))
        now = made
    y, mo = np.zeros((N, 128, C), np.float32), np.zeros((N, 8, C), np.float32)
    oc, osc = np.zeros((N, 128, 4 * C), np.uint8), np.zeros((N, 16, C), np.uint8)
    for r in range(N):
        q = mx_ref.quantize(now[r])
        y[r] = mx_ref.matmul(mx_ref.quantize(v[r]), q)
        mo[r] = mate[r]
        oc[r], osc[r] = emit(q)
    return {"y": y, "mo": mo, "oc": oc, "osc": osc}

@@ -1,0 +1,371 @@
+from concourse.bass import DstId, RemoteDMATransfer
+from concourse.mybir import dt, AluOpType, ActivationFunctionType
+
+BF, F32, I32, U16, U8, MX = "bfloat16", "float32", "int32", "uint16", "uint8", "float8_e4m3fn_x4"
+STEP = [1, 2, 4]
+C, H = 320, 160
+LOW = 256
+WIN = LOW + H
+CODES = WIN + H
+
+SCRATCH = {
+    "x0": ("sbuf", [128, 4 * C], BF), "x1": ("sbuf", [128, 4 * C], BF), "x2": ("sbuf", [128, 4 * C], BF), "x3": ("sbuf", [128, 4 * C], BF),
+    "z": ("sbuf", [128, 4 * C], BF), "a": ("sbuf", [128, 4 * C], BF),
+    "et": ("sbuf", [128, 528], BF), "eo": ("sbuf", [128, 528], BF), "eq": ("sbuf", [128, 512], MX), "eqs": ("sbuf", [128, 512], U8),
+    "ut": ("sbuf", [128, 512], BF), "uq": ("sbuf", [128, 128], MX), "uqs": ("sbuf", [128, 128], U8),
+    "u2": ("sbuf", [128, 128], MX), "u2s": ("sbuf", [128, 128], U8),
+    "vt": ("sbuf", [128, 512], BF), "vq": ("sbuf", [128, 128], MX), "vqs": ("sbuf", [128, 128], U8),
+    "wq": ("sbuf", [128, 512], MX), "wqs": ("sbuf", [128, 512], U8),
+    "qx": ("sbuf", [128, C], MX), "qxs": ("sbuf", [128, C], U8),
+    "qz": ("sbuf", [128, C], MX), "qzs": ("sbuf", [128, C], U8),
+    "qu": ("sbuf", [128, H], MX), "qus": ("sbuf", [128, H], U8),
+    "ps": ("psum", [128, 4096], F32),
+    "slo": ("sbuf", [128, H], F32), "sw": ("sbuf", [128, H], F32), "gs": ("sbuf", [128, C], F32), "sc": ("sbuf", [128, H + C], F32),
+    "mli": ("sbuf", [128, 20], I32), "zf": ("sbuf", [128, 20], F32), "wk": ("sbuf", [128, 20], F32), "kf": ("sbuf", [128, 20], F32),
+    "mk": ("sbuf", [128, 20], F32), "hb": ("sbuf", [128, 20], F32), "mm": ("sbuf", [128, 20], U16),
+    "swc": ("sbuf", [128, 10], F32), "hx": ("sbuf", [128, 20], F32), "tm": ("sbuf", [128, 20], F32), "dd": ("sbuf", [128, 10], F32),
+    "ff": ("sbuf", [128, 10], F32), "nf": ("sbuf", [128, 20], F32),
+    "ident": ("sbuf", [128, CODES + 96], F32), "aown": ("sbuf", [128, WIN], F32), "wa": ("sbuf", [128, CODES], F32), "wb": ("sbuf", [128, CODES], F32),
+    "scn": ("sbuf", [128, H], F32), "lu": ("sbuf", [128, 10], U16), "su": ("sbuf", [128, H], F32), "ssu": ("sbuf", [128, H], F32), "stu": ("sbuf", [128, 10], U16),
+    "cf": ("sbuf", [128, C], F32), "csc": ("sbuf", [128, C], F32), "zo": ("sbuf", [128, 20], U16),
+    "fin": ("sbuf", [128, C], F32), "mof": ("sbuf", [128, C], F32), "yb": ("sbuf", [128, C], F32),
+    "d0": ("sbuf", [128, C], F32), "d1": ("sbuf", [128, C], F32), "tcol": ("sbuf", [128, C], F32),
+    "pix": ("sbuf", [128, 2], I32), "qi": ("sbuf", [128, 2], I32), "qf": ("sbuf", [128, 1], F32), "q1": ("sbuf", [128, 1], F32),
+    "bias": ("sbuf", [128, 1], F32), "nb": ("sbuf", [128, 1], F32), "bz": ("sbuf", [128, 1], F32),
+    "uli": ("sbuf", [128, 8], I32), "ul": ("sbuf", [128, 8], U16),
+}
+for _b in range(4):
+    SCRATCH["xp%d" % _b] = ("sbuf", [128, WIN], BF)
+    SCRATCH["b%d" % _b] = ("sbuf", [128, C], F32)
+for _r in range(3):
+    SCRATCH["nl%d" % _r] = ("sbuf", [128, 20], U16)
+    SCRATCH["np%d" % _r] = ("sbuf", [128, 20], U16)
+    SCRATCH["ql%d" % _r] = ("sbuf", [128, H], MX)
+    SCRATCH["qls%d" % _r] = ("sbuf", [128, H], U8)
+    SCRATCH["pl%d" % _r] = ("sbuf", [128, H], MX)
+    SCRATCH["pls%d" % _r] = ("sbuf", [128, H], U8)
+SEMAPHORES = ["sv", "ss", "st", "sg", "sent", "outs", "ldxl", "ldxu", "ldu", "ldm", "ldw", "ldws", "ldv"]
+for _r in range(3):
+    SEMAPHORES += ["arrl%d" % _r, "arrc%d" % _r]
+
+LO, UP = (H, C), (0, H)
+
+
+def rank_program(g, core, T, topo):
+    rank = T.rank_of(core)
+    if rank is None:
+        return
+    queues = {"v": g.vector, "s": g.scalar, "t": g.tensor, "g": g, "y": g.sync}
+    home = {"v": "sv", "s": "ss", "t": "st", "g": "sg"}
+    count = {}
+    known = {q: {} for q in queues}
+    snap = {}
+    log = {}
+
+    def meets(e, r):
+        return e[0] < r[2] and r[1] < e[1] and (e[2] is None or r[3] is None or e[2] == r[3])
+
+    def full(r):
+        return (r[0], r[1], r[2], r[3] if len(r) > 3 else None)
+
+    def hold(q, need):
+        while need:
+            best = None
+            for s, v in need:
+                covers = sum(1 for s2, v2 in need if snap[(s, v)].get(s2, 0) >= v2)
+                if best is None or covers > best[0]: best = (covers, s, v)
+            _, s, v = best
+            queues[q].wait_ge(T.sem[s], v)
+            for s2, v2 in snap[(s, v)].items():
+                if known[q].get(s2, 0) < v2: known[q][s2] = v2
+            need = [(s2, v2) for s2, v2 in need if known[q].get(s2, 0) < v2]
+
+    def waits(q, reads, writes):
+        need = set()
+        for r in reads:
+            for e in log.get(r[0], []):
+                if e[6] and meets(e, r): need.add((e[3], e[4]))
+        for r in writes:
+            for e in log.get(r[0], []):
+                if meets(e, r) and (e[6] or e[5] != q): need.add((e[3], e[4]))
+        hold(q, [(s, v) for s, v in need if known[q].get(s, 0) < v])
+
+    def record(q, reads, writes, s, v):
+        for r in writes:
+            log[r[0]] = [e for e in log.get(r[0], []) if not (r[1] <= e[0] and e[1] <= r[2] and (r[3] is None or r[3] == e[2]))]
+            log[r[0]].append((r[1], r[2], r[3], s, v, q, True))
+        for r in reads:
+            log.setdefault(r[0], []).append((r[1], r[2], r[3], s, v, q, False))
+
+    def do(q, call, reads, writes, sem=None):
+        reads, writes = [full(r) for r in reads], [full(r) for r in writes]
+        waits(q, reads, writes)
+        inc = 16 if sem else 1
+        s = sem or home[q]
+        call(queues[q]).then_inc(T.sem[s], inc)
+        count[s] = count.get(s, 0) + inc
+        snap[(s, count[s])] = dict(known[q])
+        snap[(s, count[s])][s] = count[s]
+        record(q, reads, writes, s, count[s])
+
+    def send(dst, engines, pairs, sem):
+        rid, pid, _ = topo.addr(dst)
+        m = sum(1 << e for e in engines)
+        for src, land, region in pairs:
+            waits("g", [full(region)], [])
+            g.remote_dma(land, src, T.sem[sem], T.sem.sent, pid, rid, m)
+            count["sent"] = count.get("sent", 0) + len(engines)
+
+    def arrival(regions, sem, n):
+        count[sem] = n
+        snap[(sem, n)] = {sem: n}
+        record("remote", [], [full(r) for r in regions], sem, n)
+
+    op = AluOpType
+    COPY = ActivationFunctionType.Copy
+
+    def cols(name, a, b):
+        return T[name][:, a:b]
+
+    def tt(out, in0, in1, o, reads, writes):
+        do("v", lambda q: q.tensor_tensor(out, in0, in1, o), reads, writes)
+
+    def ts(out, in0, s1, s2, o1, o2, reads, writes):
+        if o2 is None:
+            do("v", lambda q: q.tensor_scalar(out, in0, s1, None, o1), reads, writes)
+        else:
+            do("v", lambda q: q.tensor_scalar(out, in0, s1, s2, o1, o2), reads, writes)
+
+    def vcopy(out, in_, reads, writes):
+        do("v", lambda q: q.tensor_copy(out, in_), reads, writes)
+
+    def scopy(out, in_, reads, writes, scale=1.0):
+        if scale == 1.0: do("s", lambda q: q.activation(out, in_, COPY), reads, writes)
+        else: do("s", lambda q: q.activation(out, in_, COPY, scale=scale), reads, writes)
+
+    def pick(q, out, oreg, win, wn, off, a):
+        f = vcopy if q == "v" else scopy
+        f(out, T[win][:, 0:wn].indirect(T[off][:, a:a + 10]), [(win, 0, wn), (off, a, a + 10)], [oreg])
+
+    def scan(out, oreg, src, a, n):
+        do("v", lambda q: q.tensor_tensor_scan(out, T.d0[:, 0:n], T[src][:, a:a + n], 0.0, op.add, op.min), [("d0", 0, C), (src, a, a + n)], [oreg])
+
+    def entries(out, oreg, src, a, n, col):
+        ts(out, T[src][:, a + 15:a + n:16], T[col][:, 0:1], None, op.add, None, [(src, a, a + n), (col, 0, 1)], [oreg])
+
+    def quant(out, scales, tile, a, n, dst=0):
+        do("v", lambda q: q.quantize_mx(T[out][:, dst:dst + n], T[scales][:, dst:dst + n], T[tile][:, 4 * a:4 * (a + n)]),
+           [(tile, a, a + n)], [(out, dst, dst + n), (scales, dst, dst + n)])
+
+    def product(bank, w, ws, wa, x, xs, a, n):
+        do("t", lambda q: q.matmul_mx(T.ps[:, 512 * bank:512 * bank + n], T[w][:, wa:wa + 128], T[ws][:, wa:wa + 128], T[x][:, a:a + n], T[xs][:, a:a + n], True, True),
+           [(w, wa, wa + 128), (ws, wa, wa + 128), (x, a, a + n), (xs, a, a + n)], [("bank%d" % bank, 0, 512)])
+
+    def psum(bank, n):
+        return T.ps[:, 512 * bank:512 * bank + n]
+
+    def load(q, out, in_, region, sem):
+        do(q, lambda e: e.dma_start(out, in_), [], [region], sem)
+
+    load("y", cols("x0", 4 * H, 4 * C), T.x[:, 4 * H:4 * C], ("x0", H, C), "ldxl")
+    load("s", T.ut[:], T.u[:], ("ut", 0, 128), "ldu")
+    load("y", cols("x0", 0, 4 * H), T.x[:, 0:4 * H], ("x0", 0, H), "ldxu")
+    load("s", T.mli[:], T.ml[:], ("mli", 0, 20), "ldm")
+    load("y", T.wq[:].bitcast(dt.uint8), T.wc[:], ("wq", 0, 512), "ldw")
+    load("s", T.wqs[:], T.ws[:], ("wqs", 0, 512), "ldws")
+    load("y", T.vt[:], T.v[:], ("vt", 0, 128), "ldv")
+
+    do("v", lambda q: q.memset(T.eo[:], 1.0), [], [("eo", 0, 528)])
+    do("g", lambda q: q.iota(T.pix[:], [[0, 2]], 0, 1), [], [("pix", 0, 2)])
+    do("g", lambda q: q.iota(T.uli[:], [[16, 8]], 0, 0), [], [("uli", 0, 8)])
+    do("g", lambda q: q.affine_select(T.et[:], T.eo[:], [[-1, 528]], op.is_equal, 0.0, 3, 4), [("eo", 0, 528)], [("et", 0, 528)])
+    do("g", lambda q: q.iota(T.tcol[:], [[0, 20], [1, 16]], 0, 0, allow_small_or_imprecise_dtypes=True), [], [("tcol", 0, C)])
+    do("g", lambda q: q.iota(T.ident[:], [[1, CODES + 96]], 0, 0, allow_small_or_imprecise_dtypes=True), [], [("ident", 0, CODES + 96)])
+    for b in range(4):
+        do("v", lambda q: q.memset(cols("xp%d" % b, H, LOW), 0.0), [], [("xp%d" % b, H, LOW)])
+    do("v", lambda q: q.tensor_scalar(T.qi[:], T.pix[:], 15, None, op.bitwise_and), [("pix", 0, 2)], [("qi", 0, 2)])
+    vcopy(T.ul[:], T.uli[:], [("uli", 0, 8)], [("ul", 0, 8)])
+    vcopy(T.qf[:], cols("qi", 0, 1), [("qi", 0, 1)], [("qf", 0, 1)])
+    ts(T.q1[:], T.qf[:], 1.0, None, op.add, None, [("qf", 0, 1)], [("q1", 0, 1)])
+    ts(T.bias[:], T.qf[:], 14.5, 1024.0, op.is_lt, op.mult, [("qf", 0, 1)], [("bias", 0, 1)])
+    ts(T.nb[:], T.qf[:], 14.5, -1024.0, op.is_lt, op.mult, [("qf", 0, 1)], [("nb", 0, 1)])
+    ts(T.bz[:], T.bias[:], -float(LOW), None, op.add, None, [("bias", 0, 1)], [("bz", 0, 1)])
+    for b in range(4):
+        do("v", lambda q: q.quantize_mx(cols("eq", 128 * b, 128 * b + 128), cols("eqs", 128 * b, 128 * b + 128), cols("et", 3 - b, 515 - b)),
+           [("et", 0, 528)], [("eq", 128 * b, 128 * b + 128), ("eqs", 128 * b, 128 * b + 128)])
+
+    quant("uq", "uqs", "ut", 0, 128)
+    do("v", lambda q: q.tensor_copy(T.u2[:, 0:128].bitcast(dt.uint32), T.uq[:, 0:128].bitcast(dt.uint32).indirect(T.ul[:, 0:8])),
+       [("uq", 0, 128), ("ul", 0, 8)], [("u2", 0, 128)])
+    scopy(T.u2s[:, 0:128], T.uqs[:, 0:128].indirect(T.ul[:, 0:8]), [("uqs", 0, 128), ("ul", 0, 8)], [("u2s", 0, 128)])
+
+    def scores(half):
+        product(0 if half == LO else 4, "u2", "u2s", 0, "qx", "qxs", half[0], H)
+
+    def state_quant(x, half):
+        quant("qx", "qxs", x, half[0], H, half[0])
+
+    def address(half):
+        return (LOW, WIN) if half == LO else (0, H)
+
+    def plane(x, b, half):
+        a, e = address(half)
+        scopy(cols("xp%d" % b, a, e), T[x][:, 4 * half[0] + b:4 * half[1]:4], [(x, half[0], half[1], b)], [("xp%d" % b, a, e)])
+
+    def scores_low_out():
+        scopy(T.slo[:], psum(0, H), [("bank0", 0, 512)], [("slo", 0, H)])
+
+    def prepare(first):
+        less = op.is_gt if first else op.is_lt
+        ts(T.wk[:], T.zf[:], H - 0.5, -float(H), op.is_gt, op.mult, [("zf", 0, 20)], [("wk", 0, 20)])
+        ts(T.hb[:], T.zf[:], H - 0.5, T.nb[:, 0:1], less, op.add, [("zf", 0, 20), ("nb", 0, 1)], [("hb", 0, 20)])
+        tt(T.kf[:], T.zf[:], T.wk[:], op.add, [("zf", 0, 20), ("wk", 0, 20)], [("kf", 0, 20)])
+        vcopy(T.mm[:], T.kf[:], [("kf", 0, 20)], [("mm", 0, 20)])
+        ts(T.mk[:], T.kf[:], 1.0 / LOW, None, op.mult, None, [("kf", 0, 20)], [("mk", 0, 20)])
+
+    state_quant("x0", LO)
+    scores(LO)
+    state_quant("x0", UP)
+    scores(UP)
+    scores_low_out()
+    ts(T.d1[:], T.tcol[:], T.q1[:, 0:1], -1024.0, op.is_equal, op.mult, [("tcol", 0, C), ("q1", 0, 1)], [("d1", 0, C)])
+    ts(T.wb[:, 0:C], T.tcol[:], T.qf[:, 0:1], 4096.0, op.is_equal, op.mult, [("tcol", 0, C), ("qf", 0, 1)], [("wb", 0, C)])
+    tt(T.d0[:], T.wb[:, 0:C], T.d1[:], op.add, [("wb", 0, C), ("d1", 0, C)], [("d0", 0, C)])
+    vcopy(T.zf[:], T.mli[:], [("mli", 0, 20)], [("zf", 0, 20)])
+    prepare(True)
+    for half in (UP, LO):
+        for b in range(4):
+            plane("x0", b, half)
+    scopy(cols("aown", 0, LOW), cols("ident", WIN, WIN + LOW), [("ident", WIN, WIN + LOW)], [("aown", 0, LOW)])
+    scopy(cols("wa", H, CODES), cols("ident", H, CODES), [("ident", H, CODES)], [("wa", H, CODES)])
+    scopy(cols("wb", H, CODES), cols("ident", H, CODES), [("ident", H, CODES)], [("wb", H, CODES)])
+
+    for r in range(3):
+        x, xn = "x%d" % r, "x%d" % (r + 1)
+        nl, npl = "nl%d" % r, "np%d" % r
+        ql, qls, pl, pls = "ql%d" % r, "qls%d" % r, "pl%d" % r, "pls%d" % r
+        partner = T.cores[rank ^ STEP[r]]
+        engines = topo.engines(core, partner)[:8]
+        arrival([(npl, 0, 20)], "arrl%d" % r, len(engines))
+        arrival([(pl, 0, H), (pls, 0, H)], "arrc%d" % r, 2 * len(engines))
+
+        tt(T.sw[:], psum(4, H), T.slo[:], op.is_gt, [("bank4", 0, 512), ("slo", 0, H)], [("sw", 0, H)])
+        pick("s" if r else "v", cols("gs", 0, H), ("gs", 0, H), "sw", H, "mm", 0)
+        pick("v", cols("gs", H, C), ("gs", H, C), "sw", H, "mm", 10)
+        scan(cols("sc", 0, H), ("sc", 0, H), "sw", 0, H)
+        entries(T.swc[:], ("swc", 0, 10), "sc", 0, H, "bias")
+        scan(cols("sc", 2 * H, 3 * H), ("sc", 2 * H, 3 * H), "gs", H, H)
+        scan(cols("sc", H, 2 * H), ("sc", H, 2 * H), "gs", 0, H)
+        tt(T.hx[:], T.sc[:, H + 15:3 * H:16], T.hb[:], op.not_equal, [("sc", H, 3 * H), ("hb", 0, 20)], [("hx", 0, 20)])
+        tt(T.tm[:], T.hx[:], T.mk[:], op.add, [("hx", 0, 20), ("mk", 0, 20)], [("tm", 0, 20)])
+        tt(T.dd[:], cols("tm", 10, 20), cols("tm", 0, 10), op.subtract, [("tm", 0, 20)], [("dd", 0, 10)])
+        tt(T.ff[:], T.dd[:], T.swc[:], op.mult, [("dd", 0, 10), ("swc", 0, 10)], [("ff", 0, 10)])
+        tt(cols("nf", 10, 20), cols("tm", 10, 20), T.ff[:], op.subtract, [("tm", 10, 20), ("ff", 0, 10)], [("nf", 10, 20)])
+        tt(cols("nf", 0, 10), cols("tm", 0, 10), T.ff[:], op.add, [("tm", 0, 10), ("ff", 0, 10)], [("nf", 0, 10)])
+        ts(T[nl][:], T.nf[:], float(LOW), None, op.mult, None, [("nf", 0, 20)], [(nl, 0, 20)])
+        send(partner, engines, [(T[nl][:], T[npl][:], (nl, 0, 20))], "arrl%d" % r)
+
+        def sums(half):
+            for b in range(4):
+                xp = "xp%d" % b
+                o = 10 if half == LO else 0
+                tt(T.z[:, 4 * half[0] + b:4 * half[1]:4], T[xp][:, 0:WIN].indirect(T[nl][:, o:o + 10]), T[x][:, 4 * half[0] + b:4 * half[1]:4], op.add,
+                   [(xp, 0, WIN), (nl, o, o + 10), (x, half[0], half[1], b)], [("z", half[0], half[1], b)])
+            quant("qz", "qzs", "z", half[0], H, half[0])
+
+        def layer(half):
+            k = 0 if half == LO else 4
+            for b in range(4):
+                product(k + b, "wq", "wqs", 128 * b, "qz", "qzs", half[0], H)
+            for b in range(4):
+                scopy(T.a[:, 4 * half[0] + b:4 * half[1]:4], psum(k + b, H), [("bank%d" % (k + b), 0, 512)], [("a", half[0], half[1], b)], 0.015625)
+
+        sums(LO)
+        layer(LO)
+        sums(UP)
+        quant(ql, qls, "a", H, H)
+        send(partner, engines, [(T[ql][:, 0:H].bitcast(dt.uint8), T[pl][:, 0:H].bitcast(dt.uint8), (ql, 0, H)),
+                                (T[qls][:, 0:H], T[pls][:, 0:H], (qls, 0, H))], "arrc%d" % r)
+
+        pick("s", cols("aown", LOW, WIN), ("aown", LOW, WIN), "ident", WIN, npl, 0)
+        pick("s", cols("wa", 0, H), ("wa", 0, H), "aown", WIN, nl, 10)
+        pick("s", T.su[:], ("su", 0, H), "aown", WIN, nl, 0)
+        layer(UP)
+        if r == 0:
+            quant("vq", "vqs", "vt", 0, 128)
+
+        def unpack(k, q, qs, to):
+            for b in range(4):
+                product(k + b, "eq", "eqs", 128 * b, q, qs, 0, H)
+            for b in range(4):
+                scopy(cols("b%d" % b, to, to + H), psum(k + b, H), [("bank%d" % (k + b), 0, 512)], [("b%d" % b, to, to + H)])
+
+        for level in range(4):
+            scan(T.scn[:], ("scn", 0, H), "wa", 0, H)
+            entries(T.lu[:], ("lu", 0, 10), "scn", 0, H, "bias")
+            pick("v", cols("wb", 0, H), ("wb", 0, H), "wa", CODES, "lu", 0)
+            pick("v", cols("wa", 0, H), ("wa", 0, H), "wb", CODES, "lu", 0)
+            if level == 0:
+                scan(T.ssu[:], ("ssu", 0, H), "su", 0, H)
+                entries(T.stu[:], ("stu", 0, 10), "ssu", 0, H, "bias")
+            if level == 1:
+                quant("qu", "qus", "a", 0, H)
+                unpack(0, "qu", "qus", H)
+                unpack(4, pl, pls, 0)
+        pick("v", cols("cf", H, C), ("cf", H, C), "wa", CODES, npl, 10)
+        pick("s", cols("cf", 0, H), ("cf", 0, H), "wa", CODES, "stu", 0)
+        scan(cols("csc", H, C), ("csc", H, C), "cf", H, H)
+        entries(cols("zo", 10, 20), ("zo", 10, 20), "csc", H, H, "bz")
+
+        def renew(half):
+            a, e = address(half)
+            o = 10 if half == LO else 0
+            for b in range(4):
+                xp, bb = "xp%d" % b, "b%d" % b
+                tt(T[xn][:, 4 * half[0] + b:4 * half[1]:4], T[bb][:, 0:C].indirect(T.zo[:, o:o + 10]), cols(xp, a, e), op.add,
+                   [(bb, 0, C), ("zo", o, o + 10), (xp, a, e)], [(xn, half[0], half[1], b)])
+
+        last = r == 2
+        renew(LO)
+        state_quant(xn, LO)
+        if not last:
+            scores(LO)
+            for b in range(4):
+                plane(xn, b, LO)
+        else:
+            product(0, "vq", "vqs", 0, "qx", "qxs", H, H)
+        scan(cols("csc", 0, H), ("csc", 0, H), "cf", 0, H)
+        entries(cols("zo", 0, 10), ("zo", 0, 10), "csc", 0, H, "bz")
+        if last:
+            scopy(cols("fin", 0, H), cols("ident", H, C), [("ident", H, C)], [("fin", 0, H)])
+            scopy(cols("fin", H, C), cols("ident", 0, H), [("ident", 0, H)], [("fin", H, C)])
+            pick("s", cols("mof", H, C), ("mof", H, C), "fin", C, "zo", 10)
+            pick("s", cols("mof", 0, H), ("mof", 0, H), "fin", C, "zo", 0)
+        renew(UP)
+        state_quant(xn, UP)
+        if not last:
+            scores(UP)
+            plane(xn, 0, UP)
+            plane(xn, 1, UP)
+            scores_low_out()
+            plane(xn, 2, UP)
+            plane(xn, 3, UP)
+            ts(T.zf[:], T.csc[:, 15:C:16], T.bz[:, 0:1], None, op.add, None, [("csc", 0, C), ("bz", 0, 1)], [("zf", 0, 20)])
+            prepare(False)
+        else:
+            product(4, "vq", "vqs", 0, "qx", "qxs", 0, H)
+
+    def store(q, out, in_, region):
+        do(q, lambda e: e.dma_start(out, in_), [region], [], "outs")
+
+    store("y", T.oc[:, 4 * H:4 * C], cols("qx", H, C).bitcast(dt.uint8), ("qx", H, C))
+    store("y", T.mo[:], T.mof[0:128:16, :], ("mof", 0, C))
+    scopy(cols("yb", H, C), psum(0, H), [("bank0", 0, 512)], [("yb", H, C)])
+    store("s", T.y[:, H:C], cols("yb", H, C), ("yb", H, C))
+    store("y", T.oc[:, 0:4 * H], cols("qx", 0, H).bitcast(dt.uint8), ("qx", 0, H))
+    for k in range(4):
+        store("y", T.osc[4 * k:4 * k + 4, :], T.qxs[32 * k:32 * k + 4, 0:C], ("qxs", 0, C))
+    scopy(cols("yb", 0, H), psum(4, H), [("bank4", 0, 512)], [("yb", 0, H)])
+    store("s", T.y[:, 0:H], cols("yb", 0, H), ("yb", 0, H))
+    for s in SEMAPHORES:
+        if count.get(s, 0): g.wait_ge(T.sem[s], count[s])

@@ -1,4 +1,3 @@
-from concourse.bass import DstId, RemoteDMATransfer
 from concourse.mybir import dt, AluOpType, ActivationFunctionType
 
 BF, F32, I32, U16, U8, MX = "bfloat16", "float32", "int32", "uint16", "uint8", "float8_e4m3fn_x4"
@@ -20,31 +19,34 @@ SCRATCH = {
     "qz": ("sbuf", [128, C], MX), "qzs": ("sbuf", [128, C], U8),
     "qu": ("sbuf", [128, H], MX), "qus": ("sbuf", [128, H], U8),
     "ps": ("psum", [128, 4096], F32),
-    "slo": ("sbuf", [128, H], F32), "sw": ("sbuf", [128, H], F32), "gs": ("sbuf", [128, C], F32), "sc": ("sbuf", [128, H + C], F32),
+    "slo": ("sbuf", [128, H], F32), "sw": ("sbuf", [128, C], F32), "gs": ("sbuf", [128, C], F32), "sc": ("sbuf", [128, H + C], F32),
     "mli": ("sbuf", [128, 20], I32), "zf": ("sbuf", [128, 20], F32), "wk": ("sbuf", [128, 20], F32), "kf": ("sbuf", [128, 20], F32),
-    "mk": ("sbuf", [128, 20], F32), "hb": ("sbuf", [128, 20], F32), "mm": ("sbuf", [128, 20], U16),
-    "swc": ("sbuf", [128, 10], F32), "hx": ("sbuf", [128, 20], F32), "tm": ("sbuf", [128, 20], F32), "dd": ("sbuf", [128, 10], F32),
-    "ff": ("sbuf", [128, 10], F32), "nf": ("sbuf", [128, 20], F32),
-    "ident": ("sbuf", [128, CODES + 96], F32), "aown": ("sbuf", [128, WIN], F32), "wa": ("sbuf", [128, CODES], F32), "wb": ("sbuf", [128, CODES], F32),
-    "scn": ("sbuf", [128, H], F32), "lu": ("sbuf", [128, 10], U16), "su": ("sbuf", [128, H], F32), "ssu": ("sbuf", [128, H], F32), "stu": ("sbuf", [128, 10], U16),
+    "kb": ("sbuf", [128, 20], F32), "mm": ("sbuf", [128, 20], U16), "cc": ("sbuf", [128, 40], F32), "kc": ("sbuf", [128, 40], F32),
+    "pq": ("sbuf", [128, 40], F32), "nf": ("sbuf", [128, 20], F32),
+    "mlp": ("sbuf", [128, 20], I32), "pzf": ("sbuf", [128, 20], F32), "pkb": ("sbuf", [128, 20], F32),
+    "bits": ("sbuf", [128, 30], F32), "bitp": ("sbuf", [128, 30], F32),
+    "ident": ("sbuf", [128, WIN], F32), "aown": ("sbuf", [128, WIN], F32), "wa": ("sbuf", [128, CODES], F32), "wb": ("sbuf", [128, CODES], F32),
+    "su": ("sbuf", [128, H], F32), "ssu": ("sbuf", [128, H], F32), "stu": ("sbuf", [128, 10], U16),
     "cf": ("sbuf", [128, C], F32), "csc": ("sbuf", [128, C], F32), "zo": ("sbuf", [128, 20], U16),
     "fin": ("sbuf", [128, C], F32), "mof": ("sbuf", [128, C], F32), "yb": ("sbuf", [128, C], F32),
-    "d0": ("sbuf", [128, C], F32), "d1": ("sbuf", [128, C], F32), "tcol": ("sbuf", [128, C], F32),
-    "pix": ("sbuf", [128, 2], I32), "qi": ("sbuf", [128, 2], I32), "qf": ("sbuf", [128, 1], F32), "q1": ("sbuf", [128, 1], F32),
-    "bias": ("sbuf", [128, 1], F32), "nb": ("sbuf", [128, 1], F32), "bz": ("sbuf", [128, 1], F32),
+    "d0": ("sbuf", [128, C], F32), "ds": ("sbuf", [128, 16], F32), "d1": ("sbuf", [128, 16], F32), "d2": ("sbuf", [128, 16], F32), "tcol": ("sbuf", [128, 16], F32),
+    "pix": ("sbuf", [128, 20], I32), "qi": ("sbuf", [128, 20], I32), "qo": ("sbuf", [128, 20], U16), "qf": ("sbuf", [128, 1], F32), "q1": ("sbuf", [128, 1], F32),
+    "bias": ("sbuf", [128, 1], F32), "bm": ("sbuf", [128, 1], F32), "bz": ("sbuf", [128, 1], F32),
     "uli": ("sbuf", [128, 8], I32), "ul": ("sbuf", [128, 8], U16),
 }
 for _b in range(4):
     SCRATCH["xp%d" % _b] = ("sbuf", [128, WIN], BF)
     SCRATCH["b%d" % _b] = ("sbuf", [128, C], F32)
 for _r in range(3):
+    SCRATCH["scn%d" % _r] = ("sbuf", [128, H], F32)
+    SCRATCH["lu%d" % _r] = ("sbuf", [128, 10], U16)
     SCRATCH["nl%d" % _r] = ("sbuf", [128, 20], U16)
     SCRATCH["np%d" % _r] = ("sbuf", [128, 20], U16)
     SCRATCH["ql%d" % _r] = ("sbuf", [128, H], MX)
     SCRATCH["qls%d" % _r] = ("sbuf", [128, H], U8)
     SCRATCH["pl%d" % _r] = ("sbuf", [128, H], MX)
     SCRATCH["pls%d" % _r] = ("sbuf", [128, H], U8)
-SEMAPHORES = ["sv", "ss", "st", "sg", "sent", "outs", "ldxl", "ldxu", "ldu", "ldm", "ldw", "ldws", "ldv"]
+SEMAPHORES = ["sv", "ss", "st", "sg", "sent", "outs", "ldxl", "ldxu", "ldu", "ldm", "ldw", "ldws", "ldv", "arrm"]
 for _r in range(3):
     SEMAPHORES += ["arrl%d" % _r, "arrc%d" % _r]
 
@@ -71,7 +73,7 @@ def rank_program(g, core, T, topo):
     def hold(q, need):
         while need:
             best = None
-            for s, v in need:
+            for s, v in sorted(need):
                 covers = sum(1 for s2, v2 in need if snap[(s, v)].get(s2, 0) >= v2)
                 if best is None or covers > best[0]: best = (covers, s, v)
             _, s, v = best
@@ -157,42 +159,56 @@ def rank_program(g, core, T, topo):
         do("v", lambda q: q.quantize_mx(T[out][:, dst:dst + n], T[scales][:, dst:dst + n], T[tile][:, 4 * a:4 * (a + n)]),
            [(tile, a, a + n)], [(out, dst, dst + n), (scales, dst, dst + n)])
 
-    def product(bank, w, ws, wa, x, xs, a, n):
-        do("t", lambda q: q.matmul_mx(T.ps[:, 512 * bank:512 * bank + n], T[w][:, wa:wa + 128], T[ws][:, wa:wa + 128], T[x][:, a:a + n], T[xs][:, a:a + n], True, True),
-           [(w, wa, wa + 128), (ws, wa, wa + 128), (x, a, a + n), (xs, a, a + n)], [("bank%d" % bank, 0, 512)])
-
     def psum(bank, n):
         return T.ps[:, 512 * bank:512 * bank + n]
+
+    def product(bank, w, ws, wa, x, xs, a, n):
+        do("t", lambda q: q.matmul_mx(psum(bank, n), T[w][:, wa:wa + 128], T[ws][:, wa:wa + 128], T[x][:, a:a + n], T[xs][:, a:a + n], True, True),
+           [(w, wa, wa + 128), (ws, wa, wa + 128), (x, a, a + n), (xs, a, a + n)], [("bank%d" % bank, 0, 512)])
+
+    def evacuate(q, out, oreg, bank, scale=1.0):
+        if q == "s": scopy(out, psum(bank, H), [("bank%d" % bank, 0, 512)], [oreg], scale)
+        else: ts(out, psum(bank, H), scale, None, op.mult, None, [("bank%d" % bank, 0, 512)], [oreg])
 
     def load(q, out, in_, region, sem):
         do(q, lambda e: e.dma_start(out, in_), [], [region], sem)
 
     load("y", cols("x0", 4 * H, 4 * C), T.x[:, 4 * H:4 * C], ("x0", H, C), "ldxl")
-    load("s", T.ut[:], T.u[:], ("ut", 0, 128), "ldu")
-    load("y", cols("x0", 0, 4 * H), T.x[:, 0:4 * H], ("x0", 0, H), "ldxu")
     load("s", T.mli[:], T.ml[:], ("mli", 0, 20), "ldm")
+    load("y", cols("x0", 0, 4 * H), T.x[:, 0:4 * H], ("x0", 0, H), "ldxu")
+    load("s", T.ut[:], T.u[:], ("ut", 0, 128), "ldu")
     load("y", T.wq[:].bitcast(dt.uint8), T.wc[:], ("wq", 0, 512), "ldw")
     load("s", T.wqs[:], T.ws[:], ("wqs", 0, 512), "ldws")
     load("y", T.vt[:], T.v[:], ("vt", 0, 128), "ldv")
 
     do("v", lambda q: q.memset(T.eo[:], 1.0), [], [("eo", 0, 528)])
-    do("g", lambda q: q.iota(T.pix[:], [[0, 2]], 0, 1), [], [("pix", 0, 2)])
-    do("g", lambda q: q.iota(T.uli[:], [[16, 8]], 0, 0), [], [("uli", 0, 8)])
+    do("g", lambda q: q.iota(T.pix[:], [[0, 20]], 0, 1), [], [("pix", 0, 20)])
+    do("g", lambda q: q.iota(T.tcol[:], [[1, 16]], 0, 0, allow_small_or_imprecise_dtypes=True), [], [("tcol", 0, 16)])
     do("g", lambda q: q.affine_select(T.et[:], T.eo[:], [[-1, 528]], op.is_equal, 0.0, 3, 4), [("eo", 0, 528)], [("et", 0, 528)])
-    do("g", lambda q: q.iota(T.tcol[:], [[0, 20], [1, 16]], 0, 0, allow_small_or_imprecise_dtypes=True), [], [("tcol", 0, C)])
-    do("g", lambda q: q.iota(T.ident[:], [[1, CODES + 96]], 0, 0, allow_small_or_imprecise_dtypes=True), [], [("ident", 0, CODES + 96)])
-    for b in range(4):
-        do("v", lambda q: q.memset(cols("xp%d" % b, H, LOW), 0.0), [], [("xp%d" % b, H, LOW)])
-    do("v", lambda q: q.tensor_scalar(T.qi[:], T.pix[:], 15, None, op.bitwise_and), [("pix", 0, 2)], [("qi", 0, 2)])
-    vcopy(T.ul[:], T.uli[:], [("uli", 0, 8)], [("ul", 0, 8)])
+    do("g", lambda q: q.iota(T.uli[:], [[16, 8]], 0, 0), [], [("uli", 0, 8)])
+    do("g", lambda q: q.iota(T.ident[:], [[1, WIN]], 0, 0, allow_small_or_imprecise_dtypes=True), [], [("ident", 0, WIN)])
+    first = T.cores[rank ^ STEP[0]]
+    lanes = topo.engines(core, first)[:8]
+    arrival([("mlp", 0, 20)], "arrm", len(lanes))
+    arrival([("bitp", 0, 30)], "arrl0", len(lanes))
+    send(first, lanes, [(T.mli[:], T.mlp[:], ("mli", 0, 20))], "arrm")
+    do("v", lambda q: q.tensor_scalar(T.qi[:], T.pix[:], 15, None, op.bitwise_and), [("pix", 0, 20)], [("qi", 0, 20)])
     vcopy(T.qf[:], cols("qi", 0, 1), [("qi", 0, 1)], [("qf", 0, 1)])
+    vcopy(T.qo[:], T.qi[:], [("qi", 0, 20)], [("qo", 0, 20)])
     ts(T.q1[:], T.qf[:], 1.0, None, op.add, None, [("qf", 0, 1)], [("q1", 0, 1)])
+    ts(T.d2[:], T.tcol[:], T.qf[:, 0:1], 4096.0, op.is_equal, op.mult, [("tcol", 0, 16), ("qf", 0, 1)], [("d2", 0, 16)])
+    ts(T.d1[:], T.tcol[:], T.q1[:, 0:1], -1024.0, op.is_equal, op.mult, [("tcol", 0, 16), ("q1", 0, 1)], [("d1", 0, 16)])
+    tt(T.ds[:], T.d2[:], T.d1[:], op.add, [("d2", 0, 16), ("d1", 0, 16)], [("ds", 0, 16)])
+    scopy(T.d0[:], T.ds[:].indirect(T.qo[:, 0:20]), [("ds", 0, 16), ("qo", 0, 20)], [("d0", 0, C)])
     ts(T.bias[:], T.qf[:], 14.5, 1024.0, op.is_lt, op.mult, [("qf", 0, 1)], [("bias", 0, 1)])
-    ts(T.nb[:], T.qf[:], 14.5, -1024.0, op.is_lt, op.mult, [("qf", 0, 1)], [("nb", 0, 1)])
+    ts(T.bm[:], T.bias[:], -1.0, None, op.add, None, [("bias", 0, 1)], [("bm", 0, 1)])
     ts(T.bz[:], T.bias[:], -float(LOW), None, op.add, None, [("bias", 0, 1)], [("bz", 0, 1)])
+    vcopy(T.ul[:], T.uli[:], [("uli", 0, 8)], [("ul", 0, 8)])
     for b in range(4):
         do("v", lambda q: q.quantize_mx(cols("eq", 128 * b, 128 * b + 128), cols("eqs", 128 * b, 128 * b + 128), cols("et", 3 - b, 515 - b)),
            [("et", 0, 528)], [("eq", 128 * b, 128 * b + 128), ("eqs", 128 * b, 128 * b + 128)])
+    for b in range(4):
+        do("v", lambda q: q.memset(cols("xp%d" % b, H, LOW), 0.0), [], [("xp%d" % b, H, LOW)])
 
     quant("uq", "uqs", "ut", 0, 128)
     do("v", lambda q: q.tensor_copy(T.u2[:, 0:128].bitcast(dt.uint32), T.uq[:, 0:128].bitcast(dt.uint32).indirect(T.ul[:, 0:8])),
@@ -213,57 +229,70 @@ def rank_program(g, core, T, topo):
         scopy(cols("xp%d" % b, a, e), T[x][:, 4 * half[0] + b:4 * half[1]:4], [(x, half[0], half[1], b)], [("xp%d" % b, a, e)])
 
     def scores_low_out():
-        scopy(T.slo[:], psum(0, H), [("bank0", 0, 512)], [("slo", 0, H)])
+        evacuate("s", T.slo[:], ("slo", 0, H), 0)
 
-    def prepare(first):
-        less = op.is_gt if first else op.is_lt
-        ts(T.wk[:], T.zf[:], H - 0.5, -float(H), op.is_gt, op.mult, [("zf", 0, 20)], [("wk", 0, 20)])
-        ts(T.hb[:], T.zf[:], H - 0.5, T.nb[:, 0:1], less, op.add, [("zf", 0, 20), ("nb", 0, 1)], [("hb", 0, 20)])
-        tt(T.kf[:], T.zf[:], T.wk[:], op.add, [("zf", 0, 20), ("wk", 0, 20)], [("kf", 0, 20)])
-        vcopy(T.mm[:], T.kf[:], [("kf", 0, 20)], [("mm", 0, 20)])
-        ts(T.mk[:], T.kf[:], 1.0 / LOW, None, op.mult, None, [("kf", 0, 20)], [("mk", 0, 20)])
+    def prepare(zf="zf", kb="kb"):
+        ts(T.wk[:], T[zf][:], H - 0.5, -float(H), op.is_gt, op.mult, [(zf, 0, 20)], [("wk", 0, 20)])
+        tt(T.kf[:], T[zf][:], T.wk[:], op.add, [(zf, 0, 20), ("wk", 0, 20)], [("kf", 0, 20)])
+        ts(T[kb][:], T.kf[:], 1.0 / LOW, T.bias[:, 0:1], op.mult, op.add, [("kf", 0, 20), ("bias", 0, 1)], [(kb, 0, 20)])
+
+    def choose(bits, a, step):
+        for k, col, f in ((0, "bias", -4.0), (10, "bm", 4.0), (20, "bm", 4.0), (30, "bias", -4.0)):
+            ts(cols("cc", k, k + 10), T[bits][:, a:10 * step:step], T[col][:, 0:1], f, op.add, op.mult,
+               [(bits, 0, 10 * step), (col, 0, 1)], [("cc", k, k + 10)])
+
+    def turn(bits, a, step, kb, out):
+        n = 10 * step
+        for k in (20, 0):
+            tt(cols("kc", k, k + 20), cols("cc", k, k + 20), T[kb][:], op.add, [("cc", k, k + 20), (kb, 0, 20)], [("kc", k, k + 20)])
+        for k in (20, 0):
+            tt(cols("pq", k, k + 20), T[bits][:, n + a:3 * n:step], cols("kc", k, k + 20), op.add, [(bits, n, 3 * n), ("kc", k, k + 20)], [("pq", k, k + 20)])
+        for k in (20, 0):
+            tt(cols("nf", k // 2, k // 2 + 10), cols("pq", k, k + 10), cols("pq", k + 10, k + 20), op.max, [("pq", k, k + 20)], [("nf", k // 2, k // 2 + 10)])
+        for k in (10, 0):
+            ts(cols(out, k, k + 10), cols("nf", k, k + 10), float(LOW), None, op.mult, None, [("nf", k, k + 10)], [(out, k, k + 10)])
 
     state_quant("x0", LO)
     scores(LO)
     state_quant("x0", UP)
     scores(UP)
     scores_low_out()
-    ts(T.d1[:], T.tcol[:], T.q1[:, 0:1], -1024.0, op.is_equal, op.mult, [("tcol", 0, C), ("q1", 0, 1)], [("d1", 0, C)])
-    ts(T.wb[:, 0:C], T.tcol[:], T.qf[:, 0:1], 4096.0, op.is_equal, op.mult, [("tcol", 0, C), ("qf", 0, 1)], [("wb", 0, C)])
-    tt(T.d0[:], T.wb[:, 0:C], T.d1[:], op.add, [("wb", 0, C), ("d1", 0, C)], [("d0", 0, C)])
+    vcopy(T.mm[:], T.mli[:], [("mli", 0, 20)], [("mm", 0, 20)])
     vcopy(T.zf[:], T.mli[:], [("mli", 0, 20)], [("zf", 0, 20)])
-    prepare(True)
+    prepare()
     for half in (UP, LO):
         for b in range(4):
             plane("x0", b, half)
-    scopy(cols("aown", 0, LOW), cols("ident", WIN, WIN + LOW), [("ident", WIN, WIN + LOW)], [("aown", 0, LOW)])
-    scopy(cols("wa", H, CODES), cols("ident", H, CODES), [("ident", H, CODES)], [("wa", H, CODES)])
-    scopy(cols("wb", H, CODES), cols("ident", H, CODES), [("ident", H, CODES)], [("wb", H, CODES)])
+    do("s", lambda q: q.activation(cols("aown", 0, LOW), cols("ident", 0, LOW), ActivationFunctionType.Identity, bias=float(WIN)), [("ident", 0, LOW)], [("aown", 0, LOW)])
+    for w in ("wa", "wb"):
+        scopy(cols(w, H, WIN), cols("ident", H, WIN), [("ident", H, WIN)], [(w, H, WIN)])
+        scopy(cols(w, WIN, CODES), cols("aown", 0, H), [("aown", 0, H)], [(w, WIN, CODES)])
 
     for r in range(3):
+        last = r == 2
         x, xn = "x%d" % r, "x%d" % (r + 1)
         nl, npl = "nl%d" % r, "np%d" % r
         ql, qls, pl, pls = "ql%d" % r, "qls%d" % r, "pl%d" % r, "pls%d" % r
         partner = T.cores[rank ^ STEP[r]]
         engines = topo.engines(core, partner)[:8]
-        arrival([(npl, 0, 20)], "arrl%d" % r, len(engines))
+        if r: arrival([(npl, 0, 20)], "arrl%d" % r, len(engines))
         arrival([(pl, 0, H), (pls, 0, H)], "arrc%d" % r, 2 * len(engines))
 
-        tt(T.sw[:], psum(4, H), T.slo[:], op.is_gt, [("bank4", 0, 512), ("slo", 0, H)], [("sw", 0, H)])
-        pick("s" if r else "v", cols("gs", 0, H), ("gs", 0, H), "sw", H, "mm", 0)
-        pick("v", cols("gs", H, C), ("gs", H, C), "sw", H, "mm", 10)
-        scan(cols("sc", 0, H), ("sc", 0, H), "sw", 0, H)
-        entries(T.swc[:], ("swc", 0, 10), "sc", 0, H, "bias")
+        hi, lo = (H, 0) if r else (0, H)
+        mates = "zo" if r else "mm"
+        for k, o in ((hi, op.is_gt), (lo, op.is_le)):
+            tt(cols("sw", k, k + H), psum(4, H), T.slo[:], o, [("bank4", 0, 512), ("slo", 0, H)], [("sw", k, k + H)])
+        pick("s" if r else "v", cols("gs", 0, H), ("gs", 0, H), "sw", C, mates, 0)
+        pick("v", cols("gs", H, C), ("gs", H, C), "sw", C, mates, 10)
+        scan(cols("sc", 0, H), ("sc", 0, H), "sw", hi, H)
         scan(cols("sc", 2 * H, 3 * H), ("sc", 2 * H, 3 * H), "gs", H, H)
+        choose("sc", 15, 16)
         scan(cols("sc", H, 2 * H), ("sc", H, 2 * H), "gs", 0, H)
-        tt(T.hx[:], T.sc[:, H + 15:3 * H:16], T.hb[:], op.not_equal, [("sc", H, 3 * H), ("hb", 0, 20)], [("hx", 0, 20)])
-        tt(T.tm[:], T.hx[:], T.mk[:], op.add, [("hx", 0, 20), ("mk", 0, 20)], [("tm", 0, 20)])
-        tt(T.dd[:], cols("tm", 10, 20), cols("tm", 0, 10), op.subtract, [("tm", 0, 20)], [("dd", 0, 10)])
-        tt(T.ff[:], T.dd[:], T.swc[:], op.mult, [("dd", 0, 10), ("swc", 0, 10)], [("ff", 0, 10)])
-        tt(cols("nf", 10, 20), cols("tm", 10, 20), T.ff[:], op.subtract, [("tm", 10, 20), ("ff", 0, 10)], [("nf", 10, 20)])
-        tt(cols("nf", 0, 10), cols("tm", 0, 10), T.ff[:], op.add, [("tm", 0, 10), ("ff", 0, 10)], [("nf", 0, 10)])
-        ts(T[nl][:], T.nf[:], float(LOW), None, op.mult, None, [("nf", 0, 20)], [(nl, 0, 20)])
-        send(partner, engines, [(T[nl][:], T[npl][:], (nl, 0, 20))], "arrl%d" % r)
+        if r == 0:
+            vcopy(T.bits[:], T.sc[:, 15:3 * H:16], [("sc", 0, 3 * H)], [("bits", 0, 30)])
+            send(partner, engines, [(T.bits[:], T.bitp[:], ("bits", 0, 30))], "arrl0")
+        turn("sc", 15, 16, "kb", nl)
+        if r: send(partner, engines, [(T[nl][:], T[npl][:], (nl, 0, 20))], "arrl%d" % r)
 
         def sums(half):
             for b in range(4):
@@ -273,60 +302,80 @@ def rank_program(g, core, T, topo):
                    [(xp, 0, WIN), (nl, o, o + 10), (x, half[0], half[1], b)], [("z", half[0], half[1], b)])
             quant("qz", "qzs", "z", half[0], H, half[0])
 
-        def layer(half):
-            k = 0 if half == LO else 4
+        def layer(k, half):
             for b in range(4):
                 product(k + b, "wq", "wqs", 128 * b, "qz", "qzs", half[0], H)
-            for b in range(4):
-                scopy(T.a[:, 4 * half[0] + b:4 * half[1]:4], psum(k + b, H), [("bank%d" % (k + b), 0, 512)], [("a", half[0], half[1], b)], 0.015625)
+
+        def made(q, b, k, half):
+            evacuate(q, T.a[:, 4 * half[0] + b:4 * half[1]:4], ("a", half[0], half[1], b), k + b, 0.015625)
 
         sums(LO)
-        layer(LO)
+        layer(0, LO)
+        for b in range(4):
+            made("s", b, 0, LO)
         sums(UP)
+        layer(4, UP)
         quant(ql, qls, "a", H, H)
         send(partner, engines, [(T[ql][:, 0:H].bitcast(dt.uint8), T[pl][:, 0:H].bitcast(dt.uint8), (ql, 0, H)),
                                 (T[qls][:, 0:H], T[pls][:, 0:H], (qls, 0, H))], "arrc%d" % r)
+        if r == 0:
+            quant("vq", "vqs", "vt", 0, 128)
+            vcopy(T.pzf[:], T.mlp[:], [("mlp", 0, 20)], [("pzf", 0, 20)])
+            prepare("pzf", "pkb")
+            choose("bitp", 0, 1)
+            turn("bitp", 0, 1, "pkb", npl)
 
         pick("s", cols("aown", LOW, WIN), ("aown", LOW, WIN), "ident", WIN, npl, 0)
         pick("s", cols("wa", 0, H), ("wa", 0, H), "aown", WIN, nl, 10)
-        pick("s", T.su[:], ("su", 0, H), "aown", WIN, nl, 0)
-        layer(UP)
-        if r == 0:
-            quant("vq", "vqs", "vt", 0, 128)
 
-        def unpack(k, q, qs, to):
+        def unpack(k, q, qs):
             for b in range(4):
                 product(k + b, "eq", "eqs", 128 * b, q, qs, 0, H)
-            for b in range(4):
-                scopy(cols("b%d" % b, to, to + H), psum(k + b, H), [("bank%d" % (k + b), 0, 512)], [("b%d" % b, to, to + H)])
 
-        for level in range(4):
-            scan(T.scn[:], ("scn", 0, H), "wa", 0, H)
-            entries(T.lu[:], ("lu", 0, 10), "scn", 0, H, "bias")
-            pick("v", cols("wb", 0, H), ("wb", 0, H), "wa", CODES, "lu", 0)
-            pick("v", cols("wa", 0, H), ("wa", 0, H), "wb", CODES, "lu", 0)
-            if level == 0:
-                scan(T.ssu[:], ("ssu", 0, H), "su", 0, H)
-                entries(T.stu[:], ("stu", 0, 10), "ssu", 0, H, "bias")
-            if level == 1:
+        def unpacked(q, b, k, to):
+            evacuate(q, cols("b%d" % b, to, to + H), ("b%d" % b, to, to + H), k + b)
+
+        def beside(k):
+            if k < 4: made("v", k, 4, UP)
+            elif k == 4:
                 quant("qu", "qus", "a", 0, H)
-                unpack(0, "qu", "qus", H)
-                unpack(4, pl, pls, 0)
-        pick("v", cols("cf", H, C), ("cf", H, C), "wa", CODES, npl, 10)
-        pick("s", cols("cf", 0, H), ("cf", 0, H), "wa", CODES, "stu", 0)
-        scan(cols("csc", H, C), ("csc", H, C), "cf", H, H)
-        entries(cols("zo", 10, 20), ("zo", 10, 20), "csc", H, H, "bz")
+                unpack(0, "qu", "qus")
+            else: unpacked("v", k - 5, 0, H)
 
-        def renew(half):
+        win, nxt = "wa", "wb"
+        for k in range(9):
+            if k < 8:
+                scn, lu = "scn%d" % (k % 3), "lu%d" % (k % 3)
+                scan(T[scn][:], (scn, 0, H), win, 0, H)
+                beside(k)
+                entries(T[lu][:], (lu, 0, 10), scn, 0, H, "bias")
+            pick("s", cols(nxt, 0, H), (nxt, 0, H), win, CODES, "lu%d" % (max(k - 1, 0) % 3), 0)
+            if k == 1: pick("s", T.su[:], ("su", 0, H), "aown", WIN, nl, 0)
+            win, nxt = nxt, win
+        unpacked("s", 3, 0, H)
+        scan(T.ssu[:], ("ssu", 0, H), "su", 0, H)
+        entries(T.stu[:], ("stu", 0, 10), "ssu", 0, H, "bias")
+        unpack(4, pl, pls)
+        pick("v", cols("cf", H, C), ("cf", H, C), win, CODES, npl, 10)
+        unpacked("s", 0, 4, 0)
+        unpacked("v", 2, 4, 0)
+        scan(cols("csc", H, C), ("csc", H, C), "cf", H, H)
+        unpacked("s", 1, 4, 0)
+        unpacked("v", 3, 4, 0)
+        entries(cols("zo", 10, 20), ("zo", 10, 20), "csc", H, H, "bz")
+        pick("s", cols("cf", 0, H), ("cf", 0, H), win, CODES, "stu", 0)
+
+        def renew(half, b):
             a, e = address(half)
             o = 10 if half == LO else 0
-            for b in range(4):
-                xp, bb = "xp%d" % b, "b%d" % b
-                tt(T[xn][:, 4 * half[0] + b:4 * half[1]:4], T[bb][:, 0:C].indirect(T.zo[:, o:o + 10]), cols(xp, a, e), op.add,
-                   [(bb, 0, C), ("zo", o, o + 10), (xp, a, e)], [(xn, half[0], half[1], b)])
+            xp, bb = "xp%d" % b, "b%d" % b
+            tt(T[xn][:, 4 * half[0] + b:4 * half[1]:4], T[bb][:, 0:C].indirect(T.zo[:, o:o + 10]), cols(xp, a, e), op.add,
+               [(bb, 0, C), ("zo", o, o + 10), (xp, a, e)], [(xn, half[0], half[1], b)])
 
-        last = r == 2
-        renew(LO)
+        for b in range(4):
+            renew(LO, b)
+            if b == 1: scan(cols("csc", 0, H), ("csc", 0, H), "cf", 0, H)
+        entries(cols("zo", 0, 10), ("zo", 0, 10), "csc", 0, H, "bz")
         state_quant(xn, LO)
         if not last:
             scores(LO)
@@ -334,14 +383,12 @@ def rank_program(g, core, T, topo):
                 plane(xn, b, LO)
         else:
             product(0, "vq", "vqs", 0, "qx", "qxs", H, H)
-        scan(cols("csc", 0, H), ("csc", 0, H), "cf", 0, H)
-        entries(cols("zo", 0, 10), ("zo", 0, 10), "csc", 0, H, "bz")
-        if last:
             scopy(cols("fin", 0, H), cols("ident", H, C), [("ident", H, C)], [("fin", 0, H)])
             scopy(cols("fin", H, C), cols("ident", 0, H), [("ident", 0, H)], [("fin", H, C)])
             pick("s", cols("mof", H, C), ("mof", H, C), "fin", C, "zo", 10)
             pick("s", cols("mof", 0, H), ("mof", 0, H), "fin", C, "zo", 0)
-        renew(UP)
+        for b in range(4):
+            renew(UP, b)
         state_quant(xn, UP)
         if not last:
             scores(UP)
@@ -351,7 +398,7 @@ def rank_program(g, core, T, topo):
             plane(xn, 2, UP)
             plane(xn, 3, UP)
             ts(T.zf[:], T.csc[:, 15:C:16], T.bz[:, 0:1], None, op.add, None, [("csc", 0, C), ("bz", 0, 1)], [("zf", 0, 20)])
-            prepare(False)
+            prepare()
         else:
             product(4, "vq", "vqs", 0, "qx", "qxs", 0, H)
 
@@ -360,12 +407,12 @@ def rank_program(g, core, T, topo):
 
     store("y", T.oc[:, 4 * H:4 * C], cols("qx", H, C).bitcast(dt.uint8), ("qx", H, C))
     store("y", T.mo[:], T.mof[0:128:16, :], ("mof", 0, C))
-    scopy(cols("yb", H, C), psum(0, H), [("bank0", 0, 512)], [("yb", H, C)])
+    evacuate("s", cols("yb", H, C), ("yb", H, C), 0)
     store("s", T.y[:, H:C], cols("yb", H, C), ("yb", H, C))
     store("y", T.oc[:, 0:4 * H], cols("qx", 0, H).bitcast(dt.uint8), ("qx", 0, H))
     for k in range(4):
         store("y", T.osc[4 * k:4 * k + 4, :], T.qxs[32 * k:32 * k + 4, 0:C], ("qxs", 0, C))
-    scopy(cols("yb", 0, H), psum(4, H), [("bank4", 0, 512)], [("yb", 0, H)])
+    evacuate("s", cols("yb", 0, H), ("yb", 0, H), 4)
     store("s", T.y[:, 0:H], cols("yb", 0, H), ("yb", 0, H))
     for s in SEMAPHORES:
         if count.get(s, 0): g.wait_ge(T.sem[s], count[s])

@@ -19,9 +19,9 @@ SCRATCH = {
     "qz": ("sbuf", [128, C], MX), "qzs": ("sbuf", [128, C], U8),
     "qu": ("sbuf", [128, H], MX), "qus": ("sbuf", [128, H], U8),
     "ps": ("psum", [128, 4096], F32),
-    "slo": ("sbuf", [128, H], F32), "sw": ("sbuf", [128, C], F32), "gs": ("sbuf", [128, C], F32), "sc": ("sbuf", [128, H + C], F32),
+    "slo": ("sbuf", [128, H], F32), "sw": ("sbuf", [128, C], BF), "gs": ("sbuf", [128, C], BF), "sc": ("sbuf", [128, H + C], BF),
     "mli": ("sbuf", [128, 20], I32), "zf": ("sbuf", [128, 20], F32), "wk": ("sbuf", [128, 20], F32), "kf": ("sbuf", [128, 20], F32),
-    "kb": ("sbuf", [128, 20], F32), "mm": ("sbuf", [128, 20], U16), "cc": ("sbuf", [128, 40], F32), "kc": ("sbuf", [128, 40], F32),
+    "kb": ("sbuf", [128, 20], F32), "mm": ("sbuf", [128, 20], U16), "cc": ("sbuf", [128, 30], F32), "kc": ("sbuf", [128, 40], F32),
     "pq": ("sbuf", [128, 40], F32), "nf": ("sbuf", [128, 20], F32),
     "mlp": ("sbuf", [128, 20], I32), "pzf": ("sbuf", [128, 20], F32), "pkb": ("sbuf", [128, 20], F32),
     "bits": ("sbuf", [128, 30], F32), "bitp": ("sbuf", [128, 30], F32),
@@ -31,7 +31,8 @@ SCRATCH = {
     "fin": ("sbuf", [128, C], F32), "mof": ("sbuf", [128, C], F32), "yb": ("sbuf", [128, C], F32),
     "d0": ("sbuf", [128, C], F32), "ds": ("sbuf", [128, 16], F32), "d1": ("sbuf", [128, 16], F32), "d2": ("sbuf", [128, 16], F32), "tcol": ("sbuf", [128, 16], F32),
     "pix": ("sbuf", [128, 20], I32), "qi": ("sbuf", [128, 20], I32), "qo": ("sbuf", [128, 20], U16), "qf": ("sbuf", [128, 1], F32), "q1": ("sbuf", [128, 1], F32),
-    "bias": ("sbuf", [128, 1], F32), "bm": ("sbuf", [128, 1], F32), "bz": ("sbuf", [128, 1], F32),
+    "e0": ("sbuf", [128, H], BF), "es": ("sbuf", [128, 16], F32), "e1": ("sbuf", [128, 16], F32), "e2": ("sbuf", [128, 16], F32),
+    "bias": ("sbuf", [128, 1], F32), "bb": ("sbuf", [128, 1], F32), "bm": ("sbuf", [128, 1], F32), "bz": ("sbuf", [128, 1], F32),
     "uli": ("sbuf", [128, 8], I32), "ul": ("sbuf", [128, 8], U16),
 }
 for _b in range(4):
@@ -152,6 +153,14 @@ def rank_program(g, core, T, topo):
     def scan(out, oreg, src, a, n):
         do("v", lambda q: q.tensor_tensor_scan(out, T.d0[:, 0:n], T[src][:, a:a + n], 0.0, op.add, op.min), [("d0", 0, C), (src, a, a + n)], [oreg])
 
+    def scan_bits(a, src, b):
+        do("v", lambda q: q.tensor_tensor_scan(cols("sc", a, a + H), T.e0[:], T[src][:, b:b + H], 0.0, op.add, op.min), [("e0", 0, H), (src, b, b + H)], [("sc", a, a + H)])
+
+    def pick2(name, o, win, wn, off, a):
+        for q, c, d in (("v", 0, 6), ("s", 6, 10)):
+            f = vcopy if q == "v" else scopy
+            f(cols(name, o + 16 * c, o + 16 * d), T[win][:, 0:wn].indirect(T[off][:, a + c:a + d]), [(win, 0, wn), (off, a + c, a + d)], [(name, o + 16 * c, o + 16 * d)])
+
     def entries(out, oreg, src, a, n, col):
         ts(out, T[src][:, a + 15:a + n:16], T[col][:, 0:1], None, op.add, None, [(src, a, a + n), (col, 0, 1)], [oreg])
 
@@ -201,19 +210,20 @@ def rank_program(g, core, T, topo):
     tt(T.ds[:], T.d2[:], T.d1[:], op.add, [("d2", 0, 16), ("d1", 0, 16)], [("ds", 0, 16)])
     scopy(T.d0[:], T.ds[:].indirect(T.qo[:, 0:20]), [("ds", 0, 16), ("qo", 0, 20)], [("d0", 0, C)])
     ts(T.bias[:], T.qf[:], 14.5, 1024.0, op.is_lt, op.mult, [("qf", 0, 1)], [("bias", 0, 1)])
-    ts(T.bm[:], T.bias[:], -1.0, None, op.add, None, [("bias", 0, 1)], [("bm", 0, 1)])
+    ts(T.e2[:], T.tcol[:], T.qf[:, 0:1], 8.0, op.is_equal, op.mult, [("tcol", 0, 16), ("qf", 0, 1)], [("e2", 0, 16)])
+    ts(T.e1[:], T.tcol[:], T.q1[:, 0:1], -2.0, op.is_equal, op.mult, [("tcol", 0, 16), ("q1", 0, 1)], [("e1", 0, 16)])
+    ts(T.bb[:], T.qf[:], 14.5, 2.0, op.is_lt, op.mult, [("qf", 0, 1)], [("bb", 0, 1)])
+    tt(T.es[:], T.e2[:], T.e1[:], op.add, [("e2", 0, 16), ("e1", 0, 16)], [("es", 0, 16)])
+    scopy(T.e0[:], T.es[:].indirect(T.qo[:, 0:10]), [("es", 0, 16), ("qo", 0, 10)], [("e0", 0, H)])
+    ts(T.bm[:], T.bb[:], -1.0, None, op.add, None, [("bb", 0, 1)], [("bm", 0, 1)])
     ts(T.bz[:], T.bias[:], -float(LOW), None, op.add, None, [("bias", 0, 1)], [("bz", 0, 1)])
     vcopy(T.ul[:], T.uli[:], [("uli", 0, 8)], [("ul", 0, 8)])
     for b in range(4):
-        do("v", lambda q: q.quantize_mx(cols("eq", 128 * b, 128 * b + 128), cols("eqs", 128 * b, 128 * b + 128), cols("et", 3 - b, 515 - b)),
-           [("et", 0, 528)], [("eq", 128 * b, 128 * b + 128), ("eqs", 128 * b, 128 * b + 128)])
-    for b in range(4):
         do("v", lambda q: q.memset(cols("xp%d" % b, H, LOW), 0.0), [], [("xp%d" % b, H, LOW)])
 
-    quant("uq", "uqs", "ut", 0, 128)
-    do("v", lambda q: q.tensor_copy(T.u2[:, 0:128].bitcast(dt.uint32), T.uq[:, 0:128].bitcast(dt.uint32).indirect(T.ul[:, 0:8])),
-       [("uq", 0, 128), ("ul", 0, 8)], [("u2", 0, 128)])
-    scopy(T.u2s[:, 0:128], T.uqs[:, 0:128].indirect(T.ul[:, 0:8]), [("uqs", 0, 128), ("ul", 0, 8)], [("u2s", 0, 128)])
+    def unit(b):
+        do("v", lambda q: q.quantize_mx(cols("eq", 128 * b, 128 * b + 128), cols("eqs", 128 * b, 128 * b + 128), cols("et", 3 - b, 515 - b)),
+           [("et", 0, 528)], [("eq", 128 * b, 128 * b + 128), ("eqs", 128 * b, 128 * b + 128)])
 
     def scores(half):
         product(0 if half == LO else 4, "u2", "u2s", 0, "qx", "qxs", half[0], H)
@@ -232,19 +242,21 @@ def rank_program(g, core, T, topo):
         evacuate("s", T.slo[:], ("slo", 0, H), 0)
 
     def prepare(zf="zf", kb="kb"):
-        ts(T.wk[:], T[zf][:], H - 0.5, -float(H), op.is_gt, op.mult, [(zf, 0, 20)], [("wk", 0, 20)])
-        tt(T.kf[:], T[zf][:], T.wk[:], op.add, [(zf, 0, 20), ("wk", 0, 20)], [("kf", 0, 20)])
-        ts(T[kb][:], T.kf[:], 1.0 / LOW, T.bias[:, 0:1], op.mult, op.add, [("kf", 0, 20), ("bias", 0, 1)], [(kb, 0, 20)])
+        return [lambda: ts(T.wk[:], T[zf][:], H - 0.5, -float(H), op.is_gt, op.mult, [(zf, 0, 20)], [("wk", 0, 20)]),
+                lambda: tt(T.kf[:], T[zf][:], T.wk[:], op.add, [(zf, 0, 20), ("wk", 0, 20)], [("kf", 0, 20)]),
+                lambda: ts(T[kb][:], T.kf[:], 1.0 / LOW, T.bb[:, 0:1], op.mult, op.add, [("kf", 0, 20), ("bb", 0, 1)], [(kb, 0, 20)])]
 
     def choose(bits, a, step):
-        for k, col, f in ((0, "bias", -4.0), (10, "bm", 4.0), (20, "bm", 4.0), (30, "bias", -4.0)):
+        for k, col, f in ((10, "bm", 4.0), (20, "bb", -4.0), (0, "bb", -4.0)):
             ts(cols("cc", k, k + 10), T[bits][:, a:10 * step:step], T[col][:, 0:1], f, op.add, op.mult,
                [(bits, 0, 10 * step), (col, 0, 1)], [("cc", k, k + 10)])
 
-    def turn(bits, a, step, kb, out):
+    def blend(kb):
+        for k in (10, 0):
+            tt(cols("kc", 2 * k, 2 * k + 20), cols("cc", k, k + 20), T[kb][:], op.add, [("cc", k, k + 20), (kb, 0, 20)], [("kc", 2 * k, 2 * k + 20)])
+
+    def turn(bits, a, step, out):
         n = 10 * step
-        for k in (20, 0):
-            tt(cols("kc", k, k + 20), cols("cc", k, k + 20), T[kb][:], op.add, [("cc", k, k + 20), (kb, 0, 20)], [("kc", k, k + 20)])
         for k in (20, 0):
             tt(cols("pq", k, k + 20), T[bits][:, n + a:3 * n:step], cols("kc", k, k + 20), op.add, [(bits, n, 3 * n), ("kc", k, k + 20)], [("pq", k, k + 20)])
         for k in (20, 0):
@@ -252,21 +264,24 @@ def rank_program(g, core, T, topo):
         for k in (10, 0):
             ts(cols(out, k, k + 10), cols("nf", k, k + 10), float(LOW), None, op.mult, None, [("nf", k, k + 10)], [(out, k, k + 10)])
 
+    vcopy(T.zf[:], T.mli[:], [("mli", 0, 20)], [("zf", 0, 20)])
+    vcopy(T.mm[:], T.mli[:], [("mli", 0, 20)], [("mm", 0, 20)])
+    for f in prepare():
+        f()
+    unit(0)
+    quant("uq", "uqs", "ut", 0, 128)
+    do("v", lambda q: q.tensor_copy(T.u2[:, 0:128].bitcast(dt.uint32), T.uq[:, 0:128].bitcast(dt.uint32).indirect(T.ul[:, 0:8])),
+       [("uq", 0, 128), ("ul", 0, 8)], [("u2", 0, 128)])
+    scopy(T.u2s[:, 0:128], T.uqs[:, 0:128].indirect(T.ul[:, 0:8]), [("uqs", 0, 128), ("ul", 0, 8)], [("u2s", 0, 128)])
     state_quant("x0", LO)
     scores(LO)
     state_quant("x0", UP)
     scores(UP)
     scores_low_out()
-    vcopy(T.mm[:], T.mli[:], [("mli", 0, 20)], [("mm", 0, 20)])
-    vcopy(T.zf[:], T.mli[:], [("mli", 0, 20)], [("zf", 0, 20)])
-    prepare()
-    for half in (UP, LO):
-        for b in range(4):
-            plane("x0", b, half)
-    do("s", lambda q: q.activation(cols("aown", 0, LOW), cols("ident", 0, LOW), ActivationFunctionType.Identity, bias=float(WIN)), [("ident", 0, LOW)], [("aown", 0, LOW)])
-    for w in ("wa", "wb"):
-        scopy(cols(w, H, WIN), cols("ident", H, WIN), [("ident", H, WIN)], [(w, H, WIN)])
-        scopy(cols(w, WIN, CODES), cols("aown", 0, H), [("aown", 0, H)], [(w, WIN, CODES)])
+    unit(1)
+    planes = [(b, half) for b in range(4) for half in (UP, LO)]
+    for b, half in planes[:3]:
+        plane("x0", b, half)
 
     for r in range(3):
         last = r == 2
@@ -282,25 +297,31 @@ def rank_program(g, core, T, topo):
         mates = "zo" if r else "mm"
         for k, o in ((hi, op.is_gt), (lo, op.is_le)):
             tt(cols("sw", k, k + H), psum(4, H), T.slo[:], o, [("bank4", 0, 512), ("slo", 0, H)], [("sw", k, k + H)])
-        pick("s" if r else "v", cols("gs", 0, H), ("gs", 0, H), "sw", C, mates, 0)
-        pick("v", cols("gs", H, C), ("gs", H, C), "sw", C, mates, 10)
-        scan(cols("sc", 0, H), ("sc", 0, H), "sw", hi, H)
-        scan(cols("sc", 2 * H, 3 * H), ("sc", 2 * H, 3 * H), "gs", H, H)
+        pick("s", cols("gs", H, C), ("gs", H, C), "sw", C, mates, 10)
+        pick("s", cols("gs", 0, H), ("gs", 0, H), "sw", C, mates, 0)
+        if r == 0:
+            for b, half in planes[3:]:
+                plane("x0", b, half)
+            do("s", lambda q: q.activation(cols("aown", 0, LOW), cols("ident", 0, LOW), ActivationFunctionType.Identity, bias=float(WIN)), [("ident", 0, LOW)], [("aown", 0, LOW)])
+            for w in ("wa", "wb"):
+                scopy(cols(w, H, WIN), cols("ident", H, WIN), [("ident", H, WIN)], [(w, H, WIN)])
+                scopy(cols(w, WIN, CODES), cols("aown", 0, H), [("aown", 0, H)], [(w, WIN, CODES)])
+        scan_bits(0, "sw", hi)
         choose("sc", 15, 16)
-        scan(cols("sc", H, 2 * H), ("sc", H, 2 * H), "gs", 0, H)
+        scan_bits(2 * H, "gs", H)
+        blend("kb")
+        scan_bits(H, "gs", 0)
         if r == 0:
             vcopy(T.bits[:], T.sc[:, 15:3 * H:16], [("sc", 0, 3 * H)], [("bits", 0, 30)])
             send(partner, engines, [(T.bits[:], T.bitp[:], ("bits", 0, 30))], "arrl0")
-        turn("sc", 15, 16, "kb", nl)
+        turn("sc", 15, 16, nl)
         if r: send(partner, engines, [(T[nl][:], T[npl][:], (nl, 0, 20))], "arrl%d" % r)
 
-        def sums(half):
-            for b in range(4):
-                xp = "xp%d" % b
-                o = 10 if half == LO else 0
-                tt(T.z[:, 4 * half[0] + b:4 * half[1]:4], T[xp][:, 0:WIN].indirect(T[nl][:, o:o + 10]), T[x][:, 4 * half[0] + b:4 * half[1]:4], op.add,
-                   [(xp, 0, WIN), (nl, o, o + 10), (x, half[0], half[1], b)], [("z", half[0], half[1], b)])
-            quant("qz", "qzs", "z", half[0], H, half[0])
+        def total(half, b):
+            xp = "xp%d" % b
+            o = 10 if half == LO else 0
+            tt(T.z[:, 4 * half[0] + b:4 * half[1]:4], T[xp][:, 0:WIN].indirect(T[nl][:, o:o + 10]), T[x][:, 4 * half[0] + b:4 * half[1]:4], op.add,
+               [(xp, 0, WIN), (nl, o, o + 10), (x, half[0], half[1], b)], [("z", half[0], half[1], b)])
 
         def layer(k, half):
             for b in range(4):
@@ -309,24 +330,42 @@ def rank_program(g, core, T, topo):
         def made(q, b, k, half):
             evacuate(q, T.a[:, 4 * half[0] + b:4 * half[1]:4], ("a", half[0], half[1], b), k + b, 0.015625)
 
-        sums(LO)
+        for b in range(4):
+            total(LO, b)
+        total(UP, 0)
+        quant("qz", "qzs", "z", H, H, H)
         layer(0, LO)
         for b in range(4):
             made("s", b, 0, LO)
-        sums(UP)
+        for b in range(1, 4):
+            total(UP, b)
+        quant("qz", "qzs", "z", 0, H)
         layer(4, UP)
-        quant(ql, qls, "a", H, H)
-        send(partner, engines, [(T[ql][:, 0:H].bitcast(dt.uint8), T[pl][:, 0:H].bitcast(dt.uint8), (ql, 0, H)),
-                                (T[qls][:, 0:H], T[pls][:, 0:H], (qls, 0, H))], "arrc%d" % r)
-        if r == 0:
-            quant("vq", "vqs", "vt", 0, 128)
-            vcopy(T.pzf[:], T.mlp[:], [("mlp", 0, 20)], [("pzf", 0, 20)])
-            prepare("pzf", "pkb")
-            choose("bitp", 0, 1)
-            turn("bitp", 0, 1, "pkb", npl)
 
-        pick("s", cols("aown", LOW, WIN), ("aown", LOW, WIN), "ident", WIN, npl, 0)
-        pick("s", cols("wa", 0, H), ("wa", 0, H), "aown", WIN, nl, 10)
+        def low_codes():
+            quant(ql, qls, "a", H, H)
+            send(partner, engines, [(T[ql][:, 0:H].bitcast(dt.uint8), T[pl][:, 0:H].bitcast(dt.uint8), (ql, 0, H)),
+                                    (T[qls][:, 0:H], T[pls][:, 0:H], (qls, 0, H))], "arrc%d" % r)
+
+        if r == 0:
+            vcopy(T.pzf[:], T.mlp[:], [("mlp", 0, 20)], [("pzf", 0, 20)])
+            quant("vq", "vqs", "vt", 0, 128)
+            steps = prepare("pzf", "pkb")
+            steps[0]()
+            low_codes()
+            steps[1]()
+            steps[2]()
+            choose("bitp", 0, 1)
+            blend("pkb")
+            turn("bitp", 0, 1, npl)
+
+        pick2("aown", LOW, "ident", WIN, npl, 0)
+        if r == 0:
+            unit(2)
+            unit(3)
+        else: low_codes()
+        pick2("wa", 0, "aown", WIN, nl, 10)
+        pick("s", T.su[:], ("su", 0, H), "aown", WIN, nl, 0)
 
         def unpack(k, q, qs):
             for b in range(4):
@@ -350,13 +389,12 @@ def rank_program(g, core, T, topo):
                 beside(k)
                 entries(T[lu][:], (lu, 0, 10), scn, 0, H, "bias")
             pick("s", cols(nxt, 0, H), (nxt, 0, H), win, CODES, "lu%d" % (max(k - 1, 0) % 3), 0)
-            if k == 1: pick("s", T.su[:], ("su", 0, H), "aown", WIN, nl, 0)
             win, nxt = nxt, win
         unpacked("s", 3, 0, H)
         scan(T.ssu[:], ("ssu", 0, H), "su", 0, H)
         entries(T.stu[:], ("stu", 0, 10), "ssu", 0, H, "bias")
         unpack(4, pl, pls)
-        pick("v", cols("cf", H, C), ("cf", H, C), win, CODES, npl, 10)
+        pick2("cf", H, win, CODES, npl, 10)
         unpacked("s", 0, 4, 0)
         unpacked("v", 2, 4, 0)
         scan(cols("csc", H, C), ("csc", H, C), "cf", H, H)
@@ -376,8 +414,12 @@ def rank_program(g, core, T, topo):
             renew(LO, b)
             if b == 1: scan(cols("csc", 0, H), ("csc", 0, H), "cf", 0, H)
         entries(cols("zo", 0, 10), ("zo", 0, 10), "csc", 0, H, "bz")
+        steps = prepare()
+        if not last:
+            ts(T.zf[:], T.csc[:, 15:C:16], T.bz[:, 0:1], None, op.add, None, [("csc", 0, C), ("bz", 0, 1)], [("zf", 0, 20)])
         state_quant(xn, LO)
         if not last:
+            steps[0]()
             scores(LO)
             for b in range(4):
                 plane(xn, b, LO)
@@ -389,6 +431,8 @@ def rank_program(g, core, T, topo):
             pick("s", cols("mof", 0, H), ("mof", 0, H), "fin", C, "zo", 0)
         for b in range(4):
             renew(UP, b)
+            if b == 1 and not last: steps[1]()
+        if not last: steps[2]()
         state_quant(xn, UP)
         if not last:
             scores(UP)
@@ -397,8 +441,6 @@ def rank_program(g, core, T, topo):
             scores_low_out()
             plane(xn, 2, UP)
             plane(xn, 3, UP)
-            ts(T.zf[:], T.csc[:, 15:C:16], T.bz[:, 0:1], None, op.add, None, [("csc", 0, C), ("bz", 0, 1)], [("zf", 0, 20)])
-            prepare()
         else:
             product(4, "vq", "vqs", 0, "qx", "qxs", 0, H)
 

from concourse.mybir import dt, AluOpType, ActivationFunctionType

BF, F32, I32, U16, U8, MX = "bfloat16", "float32", "int32", "uint16", "uint8", "float8_e4m3fn_x4"
STEP = [1, 2, 4]
C, H = 320, 160
LOW = 256
WIN = LOW + H
CODES = WIN + H

SCRATCH = {
    "x0": ("sbuf", [128, 4 * C], BF), "x1": ("sbuf", [128, 4 * C], BF), "x2": ("sbuf", [128, 4 * C], BF), "x3": ("sbuf", [128, 4 * C], BF),
    "z": ("sbuf", [128, 4 * C], BF), "a": ("sbuf", [128, 4 * C], BF),
    "et": ("sbuf", [128, 528], BF), "eo": ("sbuf", [128, 528], BF), "eq": ("sbuf", [128, 512], MX), "eqs": ("sbuf", [128, 512], U8),
    "ut": ("sbuf", [128, 512], BF), "uq": ("sbuf", [128, 128], MX), "uqs": ("sbuf", [128, 128], U8),
    "u2": ("sbuf", [128, 128], MX), "u2s": ("sbuf", [128, 128], U8),
    "vt": ("sbuf", [128, 512], BF), "vq": ("sbuf", [128, 128], MX), "vqs": ("sbuf", [128, 128], U8),
    "wq": ("sbuf", [128, 512], MX), "wqs": ("sbuf", [128, 512], U8),
    "qx": ("sbuf", [128, C], MX), "qxs": ("sbuf", [128, C], U8),
    "qz": ("sbuf", [128, C], MX), "qzs": ("sbuf", [128, C], U8),
    "qu": ("sbuf", [128, H], MX), "qus": ("sbuf", [128, H], U8),
    "ps": ("psum", [128, 4096], F32),
    "slo": ("sbuf", [128, H], F32), "sw": ("sbuf", [128, C], BF), "gs": ("sbuf", [128, C], BF), "sc": ("sbuf", [128, H + C], BF),
    "mli": ("sbuf", [128, 20], I32), "zf": ("sbuf", [128, 20], F32), "wk": ("sbuf", [128, 20], F32), "kf": ("sbuf", [128, 20], F32),
    "kb": ("sbuf", [128, 20], F32), "mm": ("sbuf", [128, 20], U16), "cc": ("sbuf", [128, 30], F32), "kc": ("sbuf", [128, 40], F32),
    "pq": ("sbuf", [128, 40], F32), "nf": ("sbuf", [128, 20], F32),
    "mlp": ("sbuf", [128, 20], I32), "pzf": ("sbuf", [128, 20], F32), "pkb": ("sbuf", [128, 20], F32),
    "bits": ("sbuf", [128, 30], F32), "bitp": ("sbuf", [128, 30], F32),
    "ident": ("sbuf", [128, WIN], F32), "aown": ("sbuf", [128, WIN], F32), "wa": ("sbuf", [128, CODES], F32), "wb": ("sbuf", [128, CODES], F32),
    "su": ("sbuf", [128, H], F32), "ssu": ("sbuf", [128, H], F32), "stu": ("sbuf", [128, 10], U16),
    "cf": ("sbuf", [128, C], F32), "csc": ("sbuf", [128, C], F32), "zo": ("sbuf", [128, 20], U16),
    "fin": ("sbuf", [128, C], F32), "mof": ("sbuf", [128, C], F32), "yb": ("sbuf", [128, C], F32),
    "d0": ("sbuf", [128, C], F32), "ds": ("sbuf", [128, 16], F32), "d1": ("sbuf", [128, 16], F32), "d2": ("sbuf", [128, 16], F32), "tcol": ("sbuf", [128, 16], F32),
    "pix": ("sbuf", [128, 20], I32), "qi": ("sbuf", [128, 20], I32), "qo": ("sbuf", [128, 20], U16), "qf": ("sbuf", [128, 1], F32), "q1": ("sbuf", [128, 1], F32),
    "e0": ("sbuf", [128, H], BF), "es": ("sbuf", [128, 16], F32), "e1": ("sbuf", [128, 16], F32), "e2": ("sbuf", [128, 16], F32),
    "bias": ("sbuf", [128, 1], F32), "bb": ("sbuf", [128, 1], F32), "bm": ("sbuf", [128, 1], F32), "bz": ("sbuf", [128, 1], F32),
    "uli": ("sbuf", [128, 8], I32), "ul": ("sbuf", [128, 8], U16),
}
for _b in range(4):
    SCRATCH["xp%d" % _b] = ("sbuf", [128, WIN], BF)
    SCRATCH["b%d" % _b] = ("sbuf", [128, C], F32)
for _r in range(3):
    SCRATCH["scn%d" % _r] = ("sbuf", [128, H], F32)
    SCRATCH["lu%d" % _r] = ("sbuf", [128, 10], U16)
    SCRATCH["nl%d" % _r] = ("sbuf", [128, 20], U16)
    SCRATCH["np%d" % _r] = ("sbuf", [128, 20], U16)
    SCRATCH["ql%d" % _r] = ("sbuf", [128, H], MX)
    SCRATCH["qls%d" % _r] = ("sbuf", [128, H], U8)
    SCRATCH["pl%d" % _r] = ("sbuf", [128, H], MX)
    SCRATCH["pls%d" % _r] = ("sbuf", [128, H], U8)
SEMAPHORES = ["sv", "ss", "st", "sg", "sent", "outs", "ldxl", "ldxu", "ldu", "ldm", "ldw", "ldws", "ldv", "arrm"]
for _r in range(3):
    SEMAPHORES += ["arrl%d" % _r, "arrc%d" % _r]

LO, UP = (H, C), (0, H)


def rank_program(g, core, T, topo):
    rank = T.rank_of(core)
    if rank is None:
        return
    queues = {"v": g.vector, "s": g.scalar, "t": g.tensor, "g": g, "y": g.sync}
    home = {"v": "sv", "s": "ss", "t": "st", "g": "sg"}
    count = {}
    known = {q: {} for q in queues}
    snap = {}
    log = {}

    def meets(e, r):
        return e[0] < r[2] and r[1] < e[1] and (e[2] is None or r[3] is None or e[2] == r[3])

    def full(r):
        return (r[0], r[1], r[2], r[3] if len(r) > 3 else None)

    def hold(q, need):
        while need:
            best = None
            for s, v in sorted(need):
                covers = sum(1 for s2, v2 in need if snap[(s, v)].get(s2, 0) >= v2)
                if best is None or covers > best[0]: best = (covers, s, v)
            _, s, v = best
            queues[q].wait_ge(T.sem[s], v)
            for s2, v2 in snap[(s, v)].items():
                if known[q].get(s2, 0) < v2: known[q][s2] = v2
            need = [(s2, v2) for s2, v2 in need if known[q].get(s2, 0) < v2]

    def waits(q, reads, writes):
        need = set()
        for r in reads:
            for e in log.get(r[0], []):
                if e[6] and meets(e, r): need.add((e[3], e[4]))
        for r in writes:
            for e in log.get(r[0], []):
                if meets(e, r) and (e[6] or e[5] != q): need.add((e[3], e[4]))
        hold(q, [(s, v) for s, v in need if known[q].get(s, 0) < v])

    def record(q, reads, writes, s, v):
        for r in writes:
            log[r[0]] = [e for e in log.get(r[0], []) if not (r[1] <= e[0] and e[1] <= r[2] and (r[3] is None or r[3] == e[2]))]
            log[r[0]].append((r[1], r[2], r[3], s, v, q, True))
        for r in reads:
            log.setdefault(r[0], []).append((r[1], r[2], r[3], s, v, q, False))

    def do(q, call, reads, writes, sem=None):
        reads, writes = [full(r) for r in reads], [full(r) for r in writes]
        waits(q, reads, writes)
        inc = 16 if sem else 1
        s = sem or home[q]
        call(queues[q]).then_inc(T.sem[s], inc)
        count[s] = count.get(s, 0) + inc
        snap[(s, count[s])] = dict(known[q])
        snap[(s, count[s])][s] = count[s]
        record(q, reads, writes, s, count[s])

    def send(dst, engines, pairs, sem):
        rid, pid, _ = topo.addr(dst)
        m = sum(1 << e for e in engines)
        for src, land, region in pairs:
            waits("g", [full(region)], [])
            g.remote_dma(land, src, T.sem[sem], T.sem.sent, pid, rid, m)
            count["sent"] = count.get("sent", 0) + len(engines)

    def arrival(regions, sem, n):
        count[sem] = n
        snap[(sem, n)] = {sem: n}
        record("remote", [], [full(r) for r in regions], sem, n)

    op = AluOpType
    COPY = ActivationFunctionType.Copy

    def cols(name, a, b):
        return T[name][:, a:b]

    def tt(out, in0, in1, o, reads, writes):
        do("v", lambda q: q.tensor_tensor(out, in0, in1, o), reads, writes)

    def ts(out, in0, s1, s2, o1, o2, reads, writes):
        if o2 is None:
            do("v", lambda q: q.tensor_scalar(out, in0, s1, None, o1), reads, writes)
        else:
            do("v", lambda q: q.tensor_scalar(out, in0, s1, s2, o1, o2), reads, writes)

    def vcopy(out, in_, reads, writes):
        do("v", lambda q: q.tensor_copy(out, in_), reads, writes)

    def scopy(out, in_, reads, writes, scale=1.0):
        if scale == 1.0: do("s", lambda q: q.activation(out, in_, COPY), reads, writes)
        else: do("s", lambda q: q.activation(out, in_, COPY, scale=scale), reads, writes)

    def pick(q, out, oreg, win, wn, off, a):
        f = vcopy if q == "v" else scopy
        f(out, T[win][:, 0:wn].indirect(T[off][:, a:a + 10]), [(win, 0, wn), (off, a, a + 10)], [oreg])

    def scan(out, oreg, src, a, n):
        do("v", lambda q: q.tensor_tensor_scan(out, T.d0[:, 0:n], T[src][:, a:a + n], 0.0, op.add, op.min), [("d0", 0, C), (src, a, a + n)], [oreg])

    def scan_bits(a, src, b):
        do("v", lambda q: q.tensor_tensor_scan(cols("sc", a, a + H), T.e0[:], T[src][:, b:b + H], 0.0, op.add, op.min), [("e0", 0, H), (src, b, b + H)], [("sc", a, a + H)])

    def pick2(name, o, win, wn, off, a):
        for q, c, d in (("v", 0, 6), ("s", 6, 10)):
            f = vcopy if q == "v" else scopy
            f(cols(name, o + 16 * c, o + 16 * d), T[win][:, 0:wn].indirect(T[off][:, a + c:a + d]), [(win, 0, wn), (off, a + c, a + d)], [(name, o + 16 * c, o + 16 * d)])

    def entries(out, oreg, src, a, n, col):
        ts(out, T[src][:, a + 15:a + n:16], T[col][:, 0:1], None, op.add, None, [(src, a, a + n), (col, 0, 1)], [oreg])

    def quant(out, scales, tile, a, n, dst=0):
        do("v", lambda q: q.quantize_mx(T[out][:, dst:dst + n], T[scales][:, dst:dst + n], T[tile][:, 4 * a:4 * (a + n)]),
           [(tile, a, a + n)], [(out, dst, dst + n), (scales, dst, dst + n)])

    def psum(bank, n):
        return T.ps[:, 512 * bank:512 * bank + n]

    def product(bank, w, ws, wa, x, xs, a, n):
        do("t", lambda q: q.matmul_mx(psum(bank, n), T[w][:, wa:wa + 128], T[ws][:, wa:wa + 128], T[x][:, a:a + n], T[xs][:, a:a + n], True, True),
           [(w, wa, wa + 128), (ws, wa, wa + 128), (x, a, a + n), (xs, a, a + n)], [("bank%d" % bank, 0, 512)])

    def evacuate(q, out, oreg, bank, scale=1.0):
        if q == "s": scopy(out, psum(bank, H), [("bank%d" % bank, 0, 512)], [oreg], scale)
        else: ts(out, psum(bank, H), scale, None, op.mult, None, [("bank%d" % bank, 0, 512)], [oreg])

    def load(q, out, in_, region, sem):
        do(q, lambda e: e.dma_start(out, in_), [], [region], sem)

    load("y", cols("x0", 4 * H, 4 * C), T.x[:, 4 * H:4 * C], ("x0", H, C), "ldxl")
    load("s", T.mli[:], T.ml[:], ("mli", 0, 20), "ldm")
    load("y", cols("x0", 0, 4 * H), T.x[:, 0:4 * H], ("x0", 0, H), "ldxu")
    load("s", T.ut[:], T.u[:], ("ut", 0, 128), "ldu")
    load("y", T.wq[:].bitcast(dt.uint8), T.wc[:], ("wq", 0, 512), "ldw")
    load("s", T.wqs[:], T.ws[:], ("wqs", 0, 512), "ldws")
    load("y", T.vt[:], T.v[:], ("vt", 0, 128), "ldv")

    do("v", lambda q: q.memset(T.eo[:], 1.0), [], [("eo", 0, 528)])
    do("g", lambda q: q.iota(T.pix[:], [[0, 20]], 0, 1), [], [("pix", 0, 20)])
    do("g", lambda q: q.iota(T.tcol[:], [[1, 16]], 0, 0, allow_small_or_imprecise_dtypes=True), [], [("tcol", 0, 16)])
    do("g", lambda q: q.affine_select(T.et[:], T.eo[:], [[-1, 528]], op.is_equal, 0.0, 3, 4), [("eo", 0, 528)], [("et", 0, 528)])
    do("g", lambda q: q.iota(T.uli[:], [[16, 8]], 0, 0), [], [("uli", 0, 8)])
    do("g", lambda q: q.iota(T.ident[:], [[1, WIN]], 0, 0, allow_small_or_imprecise_dtypes=True), [], [("ident", 0, WIN)])
    first = T.cores[rank ^ STEP[0]]
    lanes = topo.engines(core, first)[:8]
    arrival([("mlp", 0, 20)], "arrm", len(lanes))
    arrival([("bitp", 0, 30)], "arrl0", len(lanes))
    send(first, lanes, [(T.mli[:], T.mlp[:], ("mli", 0, 20))], "arrm")
    do("v", lambda q: q.tensor_scalar(T.qi[:], T.pix[:], 15, None, op.bitwise_and), [("pix", 0, 20)], [("qi", 0, 20)])
    vcopy(T.qf[:], cols("qi", 0, 1), [("qi", 0, 1)], [("qf", 0, 1)])
    vcopy(T.qo[:], T.qi[:], [("qi", 0, 20)], [("qo", 0, 20)])
    ts(T.q1[:], T.qf[:], 1.0, None, op.add, None, [("qf", 0, 1)], [("q1", 0, 1)])
    ts(T.d2[:], T.tcol[:], T.qf[:, 0:1], 4096.0, op.is_equal, op.mult, [("tcol", 0, 16), ("qf", 0, 1)], [("d2", 0, 16)])
    ts(T.d1[:], T.tcol[:], T.q1[:, 0:1], -1024.0, op.is_equal, op.mult, [("tcol", 0, 16), ("q1", 0, 1)], [("d1", 0, 16)])
    tt(T.ds[:], T.d2[:], T.d1[:], op.add, [("d2", 0, 16), ("d1", 0, 16)], [("ds", 0, 16)])
    scopy(T.d0[:], T.ds[:].indirect(T.qo[:, 0:20]), [("ds", 0, 16), ("qo", 0, 20)], [("d0", 0, C)])
    ts(T.bias[:], T.qf[:], 14.5, 1024.0, op.is_lt, op.mult, [("qf", 0, 1)], [("bias", 0, 1)])
    ts(T.e2[:], T.tcol[:], T.qf[:, 0:1], 8.0, op.is_equal, op.mult, [("tcol", 0, 16), ("qf", 0, 1)], [("e2", 0, 16)])
    ts(T.e1[:], T.tcol[:], T.q1[:, 0:1], -2.0, op.is_equal, op.mult, [("tcol", 0, 16), ("q1", 0, 1)], [("e1", 0, 16)])
    ts(T.bb[:], T.qf[:], 14.5, 2.0, op.is_lt, op.mult, [("qf", 0, 1)], [("bb", 0, 1)])
    tt(T.es[:], T.e2[:], T.e1[:], op.add, [("e2", 0, 16), ("e1", 0, 16)], [("es", 0, 16)])
    scopy(T.e0[:], T.es[:].indirect(T.qo[:, 0:10]), [("es", 0, 16), ("qo", 0, 10)], [("e0", 0, H)])
    ts(T.bm[:], T.bb[:], -1.0, None, op.add, None, [("bb", 0, 1)], [("bm", 0, 1)])
    ts(T.bz[:], T.bias[:], -float(LOW), None, op.add, None, [("bias", 0, 1)], [("bz", 0, 1)])
    vcopy(T.ul[:], T.uli[:], [("uli", 0, 8)], [("ul", 0, 8)])
    for b in range(4):
        do("v", lambda q: q.memset(cols("xp%d" % b, H, LOW), 0.0), [], [("xp%d" % b, H, LOW)])

    def unit(b):
        do("v", lambda q: q.quantize_mx(cols("eq", 128 * b, 128 * b + 128), cols("eqs", 128 * b, 128 * b + 128), cols("et", 3 - b, 515 - b)),
           [("et", 0, 528)], [("eq", 128 * b, 128 * b + 128), ("eqs", 128 * b, 128 * b + 128)])

    def scores(half):
        product(0 if half == LO else 4, "u2", "u2s", 0, "qx", "qxs", half[0], H)

    def state_quant(x, half):
        quant("qx", "qxs", x, half[0], H, half[0])

    def address(half):
        return (LOW, WIN) if half == LO else (0, H)

    def plane(x, b, half):
        a, e = address(half)
        scopy(cols("xp%d" % b, a, e), T[x][:, 4 * half[0] + b:4 * half[1]:4], [(x, half[0], half[1], b)], [("xp%d" % b, a, e)])

    def scores_low_out():
        evacuate("s", T.slo[:], ("slo", 0, H), 0)

    def prepare(zf="zf", kb="kb"):
        return [lambda: ts(T.wk[:], T[zf][:], H - 0.5, -float(H), op.is_gt, op.mult, [(zf, 0, 20)], [("wk", 0, 20)]),
                lambda: tt(T.kf[:], T[zf][:], T.wk[:], op.add, [(zf, 0, 20), ("wk", 0, 20)], [("kf", 0, 20)]),
                lambda: ts(T[kb][:], T.kf[:], 1.0 / LOW, T.bb[:, 0:1], op.mult, op.add, [("kf", 0, 20), ("bb", 0, 1)], [(kb, 0, 20)])]

    def choose(bits, a, step):
        for k, col, f in ((10, "bm", 4.0), (20, "bb", -4.0), (0, "bb", -4.0)):
            ts(cols("cc", k, k + 10), T[bits][:, a:10 * step:step], T[col][:, 0:1], f, op.add, op.mult,
               [(bits, 0, 10 * step), (col, 0, 1)], [("cc", k, k + 10)])

    def blend(kb):
        for k in (10, 0):
            tt(cols("kc", 2 * k, 2 * k + 20), cols("cc", k, k + 20), T[kb][:], op.add, [("cc", k, k + 20), (kb, 0, 20)], [("kc", 2 * k, 2 * k + 20)])

    def turn(bits, a, step, out):
        n = 10 * step
        for k in (20, 0):
            tt(cols("pq", k, k + 20), T[bits][:, n + a:3 * n:step], cols("kc", k, k + 20), op.add, [(bits, n, 3 * n), ("kc", k, k + 20)], [("pq", k, k + 20)])
        for k in (20, 0):
            tt(cols("nf", k // 2, k // 2 + 10), cols("pq", k, k + 10), cols("pq", k + 10, k + 20), op.max, [("pq", k, k + 20)], [("nf", k // 2, k // 2 + 10)])
        for k in (10, 0):
            ts(cols(out, k, k + 10), cols("nf", k, k + 10), float(LOW), None, op.mult, None, [("nf", k, k + 10)], [(out, k, k + 10)])

    vcopy(T.zf[:], T.mli[:], [("mli", 0, 20)], [("zf", 0, 20)])
    vcopy(T.mm[:], T.mli[:], [("mli", 0, 20)], [("mm", 0, 20)])
    for f in prepare():
        f()
    unit(0)
    quant("uq", "uqs", "ut", 0, 128)
    do("v", lambda q: q.tensor_copy(T.u2[:, 0:128].bitcast(dt.uint32), T.uq[:, 0:128].bitcast(dt.uint32).indirect(T.ul[:, 0:8])),
       [("uq", 0, 128), ("ul", 0, 8)], [("u2", 0, 128)])
    scopy(T.u2s[:, 0:128], T.uqs[:, 0:128].indirect(T.ul[:, 0:8]), [("uqs", 0, 128), ("ul", 0, 8)], [("u2s", 0, 128)])
    state_quant("x0", LO)
    scores(LO)
    state_quant("x0", UP)
    scores(UP)
    scores_low_out()
    unit(1)
    planes = [(b, half) for b in range(4) for half in (UP, LO)]
    for b, half in planes[:3]:
        plane("x0", b, half)

    for r in range(3):
        last = r == 2
        x, xn = "x%d" % r, "x%d" % (r + 1)
        nl, npl = "nl%d" % r, "np%d" % r
        ql, qls, pl, pls = "ql%d" % r, "qls%d" % r, "pl%d" % r, "pls%d" % r
        partner = T.cores[rank ^ STEP[r]]
        engines = topo.engines(core, partner)[:8]
        if r: arrival([(npl, 0, 20)], "arrl%d" % r, len(engines))
        arrival([(pl, 0, H), (pls, 0, H)], "arrc%d" % r, 2 * len(engines))

        hi, lo = (H, 0) if r else (0, H)
        mates = "zo" if r else "mm"
        for k, o in ((hi, op.is_gt), (lo, op.is_le)):
            tt(cols("sw", k, k + H), psum(4, H), T.slo[:], o, [("bank4", 0, 512), ("slo", 0, H)], [("sw", k, k + H)])
        pick("s", cols("gs", H, C), ("gs", H, C), "sw", C, mates, 10)
        pick("s", cols("gs", 0, H), ("gs", 0, H), "sw", C, mates, 0)
        if r == 0:
            for b, half in planes[3:]:
                plane("x0", b, half)
            do("s", lambda q: q.activation(cols("aown", 0, LOW), cols("ident", 0, LOW), ActivationFunctionType.Identity, bias=float(WIN)), [("ident", 0, LOW)], [("aown", 0, LOW)])
            for w in ("wa", "wb"):
                scopy(cols(w, H, WIN), cols("ident", H, WIN), [("ident", H, WIN)], [(w, H, WIN)])
                scopy(cols(w, WIN, CODES), cols("aown", 0, H), [("aown", 0, H)], [(w, WIN, CODES)])
        scan_bits(0, "sw", hi)
        choose("sc", 15, 16)
        scan_bits(2 * H, "gs", H)
        blend("kb")
        scan_bits(H, "gs", 0)
        if r == 0:
            vcopy(T.bits[:], T.sc[:, 15:3 * H:16], [("sc", 0, 3 * H)], [("bits", 0, 30)])
            send(partner, engines, [(T.bits[:], T.bitp[:], ("bits", 0, 30))], "arrl0")
        turn("sc", 15, 16, nl)
        if r: send(partner, engines, [(T[nl][:], T[npl][:], (nl, 0, 20))], "arrl%d" % r)

        def total(half, b):
            xp = "xp%d" % b
            o = 10 if half == LO else 0
            tt(T.z[:, 4 * half[0] + b:4 * half[1]:4], T[xp][:, 0:WIN].indirect(T[nl][:, o:o + 10]), T[x][:, 4 * half[0] + b:4 * half[1]:4], op.add,
               [(xp, 0, WIN), (nl, o, o + 10), (x, half[0], half[1], b)], [("z", half[0], half[1], b)])

        def layer(k, half):
            for b in range(4):
                product(k + b, "wq", "wqs", 128 * b, "qz", "qzs", half[0], H)

        def made(q, b, k, half):
            evacuate(q, T.a[:, 4 * half[0] + b:4 * half[1]:4], ("a", half[0], half[1], b), k + b, 0.015625)

        for b in range(4):
            total(LO, b)
        total(UP, 0)
        quant("qz", "qzs", "z", H, H, H)
        layer(0, LO)
        for b in range(4):
            made("s", b, 0, LO)
        for b in range(1, 4):
            total(UP, b)
        quant("qz", "qzs", "z", 0, H)
        layer(4, UP)

        def low_codes():
            quant(ql, qls, "a", H, H)
            send(partner, engines, [(T[ql][:, 0:H].bitcast(dt.uint8), T[pl][:, 0:H].bitcast(dt.uint8), (ql, 0, H)),
                                    (T[qls][:, 0:H], T[pls][:, 0:H], (qls, 0, H))], "arrc%d" % r)

        if r == 0:
            vcopy(T.pzf[:], T.mlp[:], [("mlp", 0, 20)], [("pzf", 0, 20)])
            quant("vq", "vqs", "vt", 0, 128)
            steps = prepare("pzf", "pkb")
            steps[0]()
            low_codes()
            steps[1]()
            steps[2]()
            choose("bitp", 0, 1)
            blend("pkb")
            turn("bitp", 0, 1, npl)

        pick2("aown", LOW, "ident", WIN, npl, 0)
        if r == 0:
            unit(2)
            unit(3)
        else: low_codes()
        pick2("wa", 0, "aown", WIN, nl, 10)
        pick("s", T.su[:], ("su", 0, H), "aown", WIN, nl, 0)

        def unpack(k, q, qs):
            for b in range(4):
                product(k + b, "eq", "eqs", 128 * b, q, qs, 0, H)

        def unpacked(q, b, k, to):
            evacuate(q, cols("b%d" % b, to, to + H), ("b%d" % b, to, to + H), k + b)

        def beside(k):
            if k < 4: made("v", k, 4, UP)
            elif k == 4:
                quant("qu", "qus", "a", 0, H)
                unpack(0, "qu", "qus")
            else: unpacked("v", k - 5, 0, H)

        win, nxt = "wa", "wb"
        for k in range(9):
            if k < 8:
                scn, lu = "scn%d" % (k % 3), "lu%d" % (k % 3)
                scan(T[scn][:], (scn, 0, H), win, 0, H)
                beside(k)
                entries(T[lu][:], (lu, 0, 10), scn, 0, H, "bias")
            pick("s", cols(nxt, 0, H), (nxt, 0, H), win, CODES, "lu%d" % (max(k - 1, 0) % 3), 0)
            win, nxt = nxt, win
        unpacked("s", 3, 0, H)
        scan(T.ssu[:], ("ssu", 0, H), "su", 0, H)
        entries(T.stu[:], ("stu", 0, 10), "ssu", 0, H, "bias")
        unpack(4, pl, pls)
        pick2("cf", H, win, CODES, npl, 10)
        unpacked("s", 0, 4, 0)
        unpacked("v", 2, 4, 0)
        scan(cols("csc", H, C), ("csc", H, C), "cf", H, H)
        unpacked("s", 1, 4, 0)
        unpacked("v", 3, 4, 0)
        entries(cols("zo", 10, 20), ("zo", 10, 20), "csc", H, H, "bz")
        pick("s", cols("cf", 0, H), ("cf", 0, H), win, CODES, "stu", 0)

        def renew(half, b):
            a, e = address(half)
            o = 10 if half == LO else 0
            xp, bb = "xp%d" % b, "b%d" % b
            tt(T[xn][:, 4 * half[0] + b:4 * half[1]:4], T[bb][:, 0:C].indirect(T.zo[:, o:o + 10]), cols(xp, a, e), op.add,
               [(bb, 0, C), ("zo", o, o + 10), (xp, a, e)], [(xn, half[0], half[1], b)])

        for b in range(4):
            renew(LO, b)
            if b == 1: scan(cols("csc", 0, H), ("csc", 0, H), "cf", 0, H)
        entries(cols("zo", 0, 10), ("zo", 0, 10), "csc", 0, H, "bz")
        steps = prepare()
        if not last:
            ts(T.zf[:], T.csc[:, 15:C:16], T.bz[:, 0:1], None, op.add, None, [("csc", 0, C), ("bz", 0, 1)], [("zf", 0, 20)])
        state_quant(xn, LO)
        if not last:
            steps[0]()
            scores(LO)
            for b in range(4):
                plane(xn, b, LO)
        else:
            product(0, "vq", "vqs", 0, "qx", "qxs", H, H)
            scopy(cols("fin", 0, H), cols("ident", H, C), [("ident", H, C)], [("fin", 0, H)])
            scopy(cols("fin", H, C), cols("ident", 0, H), [("ident", 0, H)], [("fin", H, C)])
            pick("s", cols("mof", H, C), ("mof", H, C), "fin", C, "zo", 10)
            pick("s", cols("mof", 0, H), ("mof", 0, H), "fin", C, "zo", 0)
        for b in range(4):
            renew(UP, b)
            if b == 1 and not last: steps[1]()
        if not last: steps[2]()
        state_quant(xn, UP)
        if not last:
            scores(UP)
            plane(xn, 0, UP)
            plane(xn, 1, UP)
            scores_low_out()
            plane(xn, 2, UP)
            plane(xn, 3, UP)
        else:
            product(4, "vq", "vqs", 0, "qx", "qxs", 0, H)

    def store(q, out, in_, region):
        do(q, lambda e: e.dma_start(out, in_), [region], [], "outs")

    store("y", T.oc[:, 4 * H:4 * C], cols("qx", H, C).bitcast(dt.uint8), ("qx", H, C))
    store("y", T.mo[:], T.mof[0:128:16, :], ("mof", 0, C))
    evacuate("s", cols("yb", H, C), ("yb", H, C), 0)
    store("s", T.y[:, H:C], cols("yb", H, C), ("yb", H, C))
    store("y", T.oc[:, 0:4 * H], cols("qx", 0, H).bitcast(dt.uint8), ("qx", 0, H))
    for k in range(4):
        store("y", T.osc[4 * k:4 * k + 4, :], T.qxs[32 * k:32 * k + 4, 0:C], ("qxs", 0, C))
    evacuate("s", cols("yb", 0, H), ("yb", 0, H), 4)
    store("s", T.y[:, 0:H], cols("yb", 0, H), ("yb", 0, H))
    for s in SEMAPHORES:
        if count.get(s, 0): g.wait_ge(T.sem[s], count[s])
